import numpy as np, ml_dtypes
CORES = [8,136,40,168]
N = 4
import mx_ref
BF = ml_dtypes.bfloat16
def cols(t, e):
    v = np.concatenate([t.reshape(128, -1, 4), np.zeros((128, 1, 4), BF)], axis=1)
    return np.ascontiguousarray(v[:, e]).reshape(128, -1)
def f(rng, *shape):
    return mx_ref.flush((rng.standard_normal(shape, dtype=np.float32) * np.exp2(rng.integers(-2, 3, shape[:-1] + (1,)))).astype(BF))
def wide(rng, *shape, cols=0):
    v = rng.standard_normal(shape, dtype=np.float32) * np.exp2(rng.integers(-12, 13, shape)).astype(np.float32)
    if cols: v *= np.repeat(np.exp2(rng.integers(-cols, cols + 1, shape[:-2] + (1, shape[-1] // 4))) * (rng.random(shape[:-2] + (1, shape[-1] // 4)) > 0.0625), 4, axis=-1).astype(np.float32)
    return mx_ref.flush(v.astype(BF))
T, K, O = 512, 128, 2
def setup_inputs(rng):
    u = np.zeros((128, 512), BF); u[:, :4] = f(rng, 128, 4)
    return {"x": f(rng, N, 128, 4 * T), "u": np.stack([u] * N), "w": f(rng, N, 128, 512 * O)}
def signs(d):
    return np.where(d["u"][0][:, :4].astype(np.float32) < 0, -1, 1).astype(np.float32)
def blocks(rng, n):
    return np.repeat(rng.permutation(16) < n, 8)
def plant(rng, d, n):
    for s in range(N):
        v = d["x"][s].astype(np.float32).reshape(128, T, 4)
        k = rng.permutation(T)[:n[s]]
        v[:, k] = np.abs(v[:, k]) * signs(d)[:, None] * np.float32(8)
        d["x"][s] = v.reshape(128, -1).astype(BF)
    return d
def setup_inputs_one(rng):
    d = setup_inputs(rng); return plant(rng, d, np.where(np.arange(N) == rng.integers(0, N), K, 0))
def setup_inputs_zeros(rng):
    d = setup_inputs(rng); m = blocks(rng, 2)
    d["u"][:, ~m] = 0
    k = rng.permutation(N * T); g = np.full(N * T, -1, np.float32)
    g[k[:K // 3]] = 1; g[k[K // 3:2 * (K // 3)]] = 0
    v = np.abs(d["x"][:, m].astype(np.float32)).reshape(N, -1, T, 4)
    d["x"][:, m] = (v * signs(d)[m][:, None] * g.reshape(N, 1, T, 1)).reshape(N, -1, 4 * T).astype(BF)
    return d
def setup_inputs_few(rng):
    d = setup_inputs(rng); p = rng.permutation(N); g = p[N - N // 2:]
    d["x"][g] = (-np.abs(d["x"][g].astype(np.float32)) * np.tile(signs(d), (1, T))).astype(BF)
    n = np.zeros(N, int); n[p[:2]] = [K * 3 // 5, K - K * 3 // 5]
    return plant(rng, d, n)
def setup_inputs_ties(rng):
    d = setup_inputs(rng); b = f(rng, 128, 4 * 40); m = blocks(rng, 4)
    d["u"][:, m] = 0
    d["x"] = np.stack([cols(b, rng.permutation(np.arange(T) % 40)) for r in range(N)])
    d["x"][:, m] = f(rng, N, 32, 4 * T); return d
def setup_inputs_spread(rng):
    d = setup_inputs(rng); d["x"] = wide(rng, N, 128, 4 * T, cols=8); return d
def check_inputs(d):
    b = []
    u = d["u"].astype(np.float32)
    if (u != u[:1]).any(): b.append("u_same")
    if (u[:, :, 4:] != 0).any(): b.append("u_zero")
    return b
def reference(x, u, w):
    s = np.stack([mx_ref.matmul(mx_ref.quantize(u[r]), mx_ref.quantize(x[r]))[0] for r in range(N)]).reshape(-1) + np.float32(0.0)
    best = np.lexsort((np.arange(N * T), -s))[:K]
    V = mx_ref.quantize(cols(np.concatenate(list(x), axis=1), best))
    y = np.zeros((N, 128, O * K), np.float32)
    for r in range(N):
        for o in range(O): y[r][:, K * o:K * o + K] = mx_ref.matmul(mx_ref.quantize(np.ascontiguousarray(w[r][:, 512 * o:512 * o + 512])), V)
    who = np.stack([best // T, best % T]).astype(np.float32)
    return {"y": y, "id": np.stack([who] * N)}

@@ -1,0 +1,358 @@
+from concourse.bass import DstId, RemoteDMATransfer
+from concourse.mybir import dt, AluOpType, AxisListType, ActivationFunctionType
+
+OP = AluOpType
+COPY = ActivationFunctionType.Copy
+K = 128
+BIG = 1e29
+
+SCRATCH = {
+    "ub": ("sbuf", [128, 16], "bfloat16"),
+    "ur": ("sbuf", [128, 512], "bfloat16"),
+    "uq": ("sbuf", [128, 128], "float8_e4m3fn_x4"),
+    "us": ("sbuf", [128, 128], "uint8"),
+    "xb": ("sbuf", [128, 2048], "bfloat16"),
+    "xq": ("sbuf", [128, 512], "float8_e4m3fn_x4"),
+    "xs": ("sbuf", [128, 512], "uint8"),
+    "wb": ("sbuf", [128, 1024], "bfloat16"),
+    "wq": ("sbuf", [128, 256], "float8_e4m3fn_x4"),
+    "ws": ("sbuf", [128, 256], "uint8"),
+    "c1": ("sbuf", [128, 256], "float8_e4m3fn_x4"),
+    "s1": ("sbuf", [128, 256], "uint8"),
+    "c2": ("sbuf", [128, 256], "float8_e4m3fn_x4"),
+    "s2": ("sbuf", [128, 256], "uint8"),
+    "c3": ("sbuf", [128, 128], "float8_e4m3fn_x4"),
+    "s3": ("sbuf", [128, 128], "uint8"),
+    "yb": ("sbuf", [128, 256], "float32"),
+    "psf": ("psum", [128, 2048], "float32"),
+    "psp": ("psum", [128, 2048], "float32"),
+    "ip": ("sbuf", [128, 32], "int32"), "ipa": ("sbuf", [128, 32], "int32"), "uoff": ("sbuf", [128, 32], "uint16"),
+    "it": ("sbuf", [128, 128], "int32"), "ita": ("sbuf", [128, 128], "int32"),
+    "mk": ("sbuf", [128, 128], "float32"), "nb": ("sbuf", [128, 128], "float32"),
+    "tri": ("sbuf", [128, 128], "bfloat16"),
+    "i3": ("sbuf", [128, 64], "float32"), "vals1": ("sbuf", [128, 64], "float32"),
+    "i4": ("sbuf", [128, 128], "float32"), "seg": ("sbuf", [128, 128], "float32"),
+    "i5": ("sbuf", [128, 32], "int32"), "eoff": ("sbuf", [128, 32], "uint16"),
+    "i6": ("sbuf", [128, 8], "float32"), "gm": ("sbuf", [128, 8], "float32"), "bas": ("sbuf", [128, 8], "float32"),
+    "i7": ("sbuf", [128, 32], "float32"), "hm": ("sbuf", [128, 32], "float32"),
+    "pca": ("sbuf", [128, 4], "int32"), "pcf": ("sbuf", [128, 4], "float32"),
+    "pos": ("sbuf", [128, 4], "float32"),
+    "sf": ("sbuf", [128, 512], "float32"), "sp": ("sbuf", [128, 4], "float32"),
+    "cma": ("sbuf", [128, 644], "float32"), "cmb": ("sbuf", [128, 644], "float32"),
+    "cmc": ("sbuf", [128, 644], "float32"), "cmd": ("sbuf", [128, 644], "float32"),
+    "eq": ("sbuf", [128, 512], "bfloat16"), "junk": ("sbuf", [128, 4096], "bfloat16"),
+    "pl1": ("sbuf", [128, 4], "float32"), "pl2": ("sbuf", [128, 4], "float32"),
+    "msg": ("sbuf", [128, 32], "float32"),
+    "at": ("sbuf", [128, 128], "float32"), "o1f": ("sbuf", [128, 8], "float32"), "o1g": ("sbuf", [128, 8], "float32"),
+    "am0": ("sbuf", [128, 128], "float32"), "am": ("sbuf", [128, 128], "float32"),
+    "bc": ("sbuf", [128, 128], "float32"), "bs": ("sbuf", [128, 128], "float32"),
+    "o2f": ("sbuf", [128, 8], "float32"), "off2": ("sbuf", [128, 8], "uint16"),
+    "yx": ("sbuf", [128, 512], "float32"), "fs": ("sbuf", [128, 512], "float32"),
+    "ga": ("sbuf", [128, 386], "bfloat16"), "gb": ("sbuf", [128, 386], "bfloat16"),
+    "gd": ("sbuf", [128, 386], "bfloat16"), "ge": ("sbuf", [128, 386], "bfloat16"),
+    "cp0": ("sbuf", [128, 4], "float32"), "cp": ("sbuf", [128, 4], "float32"),
+    "zx": ("sbuf", [128, 128], "float32"), "zt": ("sbuf", [128, 128], "float32"),
+    "vals2": ("sbuf", [128, 64], "float32"),
+    "pin": ("sbuf", [32, 8], "int32"), "pia": ("sbuf", [32, 8], "int32"),
+    "idn": ("sbuf", [32, 16], "int32"), "idr": ("sbuf", [32, 16], "int32"), "idc": ("sbuf", [32, 16], "int32"),
+    "idf": ("sbuf", [32, 32], "float32"),
+}
+for _n in ("1", "2"):
+    SCRATCH["pu" + _n] = ("sbuf", [128, 4], "uint16")
+    SCRATCH["win" + _n] = ("sbuf", [128, 512], "float32")
+    SCRATCH["wm" + _n] = ("sbuf", [128, 128], "float32")
+    SCRATCH["sc" + _n] = ("sbuf", [128, 128], "float32")
+    SCRATCH["qa" + _n] = ("sbuf", [64, 8], "float32")
+    for _b in ("ti", "to", "tw", "tb"):
+        SCRATCH[_b + _n] = ("sbuf", [32, 32], "float32")
+    SCRATCH["lst" + _n] = ("sbuf", [128, 8], "uint16")
+
+SEMAPHORES = ["v", "s", "t", "gc", "du", "dx0", "dx1", "dx2", "dx3", "dw", "dy0", "dy1", "did",
+              "h1c", "h1s", "h2c", "h2s", "hm", "sent"]
+
+
+def rank_program(g, core, T, topo):
+    rank = T.rank_of(core)
+    if rank is None:
+        return
+    v, s, t, y = g.vector, g.scalar, g.tensor, g.sync
+    queue = {"g": g, "v": v, "s": s, "t": t, "y": y}
+    count, waited = {}, {}
+
+    def done(ins, sem, n=1):
+        ins.then_inc(T.sem[sem], n)
+        count[sem] = count.get(sem, 0) + n
+        return (sem, count[sem])
+
+    def wait(q, *tokens):
+        for sem, n in tokens:
+            if waited.get((q, sem), 0) < n:
+                waited[(q, sem)] = n
+                queue[q].wait_ge(T.sem[sem], n)
+
+    def V(ins): return done(ins, "v")
+    def S(ins): return done(ins, "s")
+    def X(ins): return done(ins, "t")
+
+    du = done(y.dma_start(T.ub[:, 0:4], T.u[:, 0:4]), "du", 16)
+    dx = [None] * 4
+    for d in range(4):
+        q = s if d % 2 else y
+        dx[d] = done(q.dma_start(T.xb[:, 512 * d:512 * d + 512], T.x[:, 512 * d:512 * d + 512]), "dx%d" % d, 16)
+    dw = done(y.dma_start(T.wb[:, 0:1024], T.w[:, 0:1024]), "dw", 16)
+
+    def iota(buf, pattern, base, cm, flt=False):
+        if flt:
+            return done(g.iota(buf, pattern, base, cm, allow_small_or_imprecise_dtypes=True), "gc")
+        return done(g.iota(buf, pattern, base, cm), "gc")
+    k_ip = iota(T.ip[:, 0:32], [[0, 32]], 0, 1)
+    k_it = iota(T.it[:, 0:128], [[1, 128]], 128, -1)
+    k_i3 = iota(T.i3[:, 0:64], [[128, 4], [1, 16]], 0, 0, True)
+    k_i4 = iota(T.i4[:, 0:128], [[0, 8], [1, 16]], 0, 0, True)
+    k_i5 = iota(T.i5[:, 0:32], [[8, 4], [1, 4], [0, 2]], 0, 0)
+    k_i6 = iota(T.i6[:, 0:8], [[16, 8]], 0, 0, True)
+    k_i7 = iota(T.i7[:, 0:32], [[16, 2], [0, 16]], 0, 0, True)
+
+    V(v.memset(T.win1[:, 0:512], 0.0))
+    V(v.memset(T.ti1[:, 0:32], 0.0))
+    wait("v", k_ip)
+    a = V(v.tensor_scalar(T.ipa[:, 0:32], T.ip[:, 0:32], 3, None, OP.bitwise_and))
+    wait("v", a)
+    a = V(v.tensor_copy(T.uoff[:, 0:32], T.ipa[:, 0:32]))
+    V(v.tensor_scalar(T.pca[:, 0:1], T.ip[:, 0:1], 112, None, OP.bitwise_and))
+    V(v.tensor_scalar(T.pca[:, 1:2], T.ip[:, 0:1], 15, None, OP.bitwise_and))
+    V(v.tensor_scalar(T.pca[:, 2:3], T.ip[:, 0:1], 16, None, OP.bitwise_and))
+    b = V(v.tensor_copy(T.pca[:, 3:4], T.ip[:, 0:1]))
+    wait("v", b)
+    b = V(v.tensor_copy(T.pcf[:, 0:4], T.pca[:, 0:4]))
+    wait("v", k_it)
+    c = V(v.tensor_scalar(T.ita[:, 0:128], T.it[:, 0:128], 15, None, OP.bitwise_and))
+    V(v.tensor_scalar(T.tri[:, 0:128], T.it[:, 0:128], 128.0, None, OP.is_lt))
+    wait("v", c)
+    V(v.tensor_scalar(T.mk[:, 0:128], T.ita[:, 0:128], 0.0, None, OP.is_equal))
+    wait("v", b, k_i3, k_i4)
+    V(v.tensor_scalar(T.vals1[:, 0:64], T.i3[:, 0:64], T.pcf[:, 0:1], None, OP.add))
+    k_seg = V(v.tensor_scalar(T.seg[:, 0:128], T.i4[:, 0:128], 1.0, None, OP.min))
+
+    wait("v", du, a)
+    a = V(v.tensor_copy(T.ur[:, 0:512], T.ub[:, 0:4].indirect(T.uoff[:, 0:32])))
+    wait("v", a)
+    k_u = V(v.quantize_mx(T.uq[:, 0:128], T.us[:, 0:128], T.ur[:, 0:512]))
+
+    cm = [T.cma, T.cmb, T.cmc, T.cmd]
+    jk = [0]
+
+    def total(buf, lo, hi, out, *tokens):
+        wait("s", *tokens)
+        n = hi - lo
+        r = S(s.activation(T.junk[:, jk[0]:jk[0] + n], buf[:, lo:hi], COPY, accum_out=out))
+        jk[0] = jk[0] + n if jk[0] + n + 700 <= 4096 else 0
+        return r
+
+    def blk(d): return slice(128 * d, 128 * d + 128) if d < 3 else slice(513, 641)
+    early = [None] * 4
+    pl = [None] * 4
+    for d in range(4):
+        e = slice(128 * d, 128 * d + 128)
+        wait("v", dx[d])
+        kq = V(v.quantize_mx(T.xq[:, e], T.xs[:, e], T.xb[:, 512 * d:512 * d + 512]))
+        wait("t", k_u, kq)
+        kf = X(t.matmul_mx(T.psf[:, 512 * d:512 * d + 128], T.uq[:, 0:128], T.us[:, 0:128], T.xq[:, e], T.xs[:, e], True, True))
+        kp = X(t.matmul_mx(T.psp[:, 512 * d:512 * d + 128], T.xq[:, e], T.xs[:, e], T.uq[:, 0:128], T.us[:, 0:128], True, True))
+        wait("s", kf)
+        kf = S(s.activation(T.sf[:, e], T.psf[:, 512 * d:512 * d + 128], COPY))
+        wait("v", kp)
+        kp = V(v.tensor_copy(T.sp[:, d:d + 1], T.psp[:, 512 * d:512 * d + 1]))
+        wait("v", kp, kf)
+        me = T.sp[:, d:d + 1]
+        if d:
+            kge = V(v.tensor_scalar(cm[d][:, 0:128 * d], T.sf[:, 0:128 * d], me, None, OP.is_ge))
+        if d == 3:
+            early[3] = total(cm[3], 0, 384, cm[3][:, 512:513], kge)
+        low = [V(v.tensor_scalar(cm[c][:, blk(d)], T.sf[:, e], T.sp[:, c:c + 1], None, OP.is_gt)) for c in range(d)]
+        if d == 3:
+            for c in range(3):
+                pl[c] = total(cm[c], 512, 641, T.pl1[:, c:c + 1], low[c], early[c])
+        keq = V(v.tensor_scalar(T.eq[:, e], T.sf[:, e], me, None, OP.is_equal))
+        V(v.tensor_scalar(cm[d][:, blk(d)], T.sf[:, e], me, None, OP.is_gt))
+        wait("v", keq)
+        kown = V(v.tensor_tensor(cm[d][:, 384:512], T.eq[:, e], T.tri[:, 0:128], OP.mult))
+        if d == 2:
+            for c in range(3):
+                early[c] = total(cm[c], 0, 512, cm[c][:, 512:513], kown)
+        if d == 3:
+            pl[3] = total(cm[3], 384, 641, T.pl1[:, 3:4], kown, early[3])
+
+    def invert(n, places, plbuf, flip, vals, low8):
+        W = lambda b: T[b + n]
+        wait("v", *places)
+        if flip:
+            a = V(v.tensor_scalar(W("pu")[:, 0:4], plbuf[:, 0:4], -1.0, 511.0, OP.mult, OP.add))
+        else:
+            a = V(v.tensor_copy(W("pu")[:, 0:4], plbuf[:, 0:4]))
+        lo = 384 if flip else 0
+        wait("v", a)
+        a = V(v.tensor_copy(W("win")[:, 0:512].indirect(W("pu")[:, 0:4]), vals[:, 0:64]))
+        wait("v", a)
+        a = V(v.tensor_tensor(W("wm")[:, 0:128], W("win")[:, lo:lo + 128], T.mk[:, 0:128], OP.mult))
+        wait("v", a)
+        a = V(v.tensor_tensor_scan(W("sc")[:, 0:128], T.seg[:, 0:128], W("wm")[:, 0:128], 0.0, OP.mult, OP.add))
+        wait("v", a)
+        a = V(v.tensor_tensor(W("qa")[0:64, 0:8], W("sc")[0:64, 15:128:16], W("sc")[64:128, 15:128:16], OP.add))
+        wait("v", a)
+        a = V(v.tensor_tensor(W("ti")[0:32, 0:8], W("qa")[0:32, 0:8], W("qa")[32:64, 0:8], OP.add))
+        wait("v", a)
+        a = V(v.transpose(W("to")[0:32, 0:32], W("ti")[0:32, 0:32]))
+        wait("v", a)
+        V(v.tensor_tensor(W("tw")[0:32, 0:16], W("to")[0:32, 0:16], W("to")[0:32, 16:32], OP.add))
+        a = V(v.tensor_tensor(W("tw")[0:32, 16:32], W("to")[0:32, 0:16], W("to")[0:32, 16:32], OP.add))
+        wait("v", a)
+        a = V(v.transpose(W("tb")[0:32, 0:32], W("tw")[0:32, 0:32]))
+        wait("v", a)
+        src = W("tb")
+        if low8:
+            a = V(v.tensor_copy(T.pin[0:32, 0:8], W("tb")[0:32, 0:8]))
+            wait("v", a)
+            a = V(v.tensor_scalar(T.pia[0:32, 0:8], T.pin[0:32, 0:8], 255, None, OP.bitwise_and))
+            wait("v", a)
+            src = T.pia
+        for h in range(4):
+            a = V(v.tensor_copy(W("lst")[32 * h:32 * h + 32, 0:8], src[0:32, 0:8]))
+        return a
+
+    def pick(dc, ds, sc, ss, off, ready_c, ready_s):
+        wait("v", *ready_c)
+        a = V(v.tensor_copy(dc[:, 0:K].bitcast(dt.uint32), sc.bitcast(dt.uint32).indirect(off[:, 0:8])))
+        wait("s", *ready_s)
+        b = S(s.activation(ds[:, 0:K], ss.indirect(off[:, 0:8]), COPY))
+        return a, b
+
+    def send(buf_c, buf_s, a, b, dst, sem_c, sem_s):
+        rid, pid = topo.addr(dst, core)
+        m = topo.mask(core, dst)
+        n = len(topo.engines(core, dst))
+        for buf, k, sem in ((buf_c, a, sem_c), (buf_s, b, sem_s)):
+            wait("g", k)
+            o, i = buf[:, K:2 * K], buf[:, 0:K]
+            if buf is buf_c:
+                o, i = o.bitcast(dt.uint8), i.bitcast(dt.uint8)
+            g.remote_dma(o, i, T.sem[sem], T.sem["sent"], pid, rid, m)
+            count["sent"] = count.get("sent", 0) + n
+        return (sem_c, n), (sem_s, n)
+
+    k_l1 = invert("1", pl, T.pl1, rank % 2 == 1, T.vals1, False)
+    a1, b1 = pick(T.c1, T.s1, T.xq[:, 0:512], T.xs[:, 0:512], T.lst1, (k_l1,), (k_l1,))
+    mate = T.cores[rank ^ 1]
+    in1c, in1s = send(T.c1, T.s1, a1, b1, mate, "h1c", "h1s")
+
+    m0 = 8 * rank
+    wait("t", a1, b1)
+    kaf = X(t.matmul_mx(T.psf[:, 0:128], T.uq[:, 0:128], T.us[:, 0:128], T.c1[:, 0:128], T.s1[:, 0:128], True, True))
+    kap = X(t.matmul_mx(T.psp[:, 0:128], T.c1[:, 0:128], T.s1[:, 0:128], T.uq[:, 0:128], T.us[:, 0:128], True, True))
+    wait("v", k_l1, k_i6, b)
+    V(v.tensor_scalar(T.gm[:, 0:8], T.i6[:, 0:8], T.pcf[:, 0:1], None, OP.is_equal))
+    a = V(v.tensor_copy(T.o1f[:, 0:8], T.lst1[:, 0:8]))
+    wait("v", a)
+    a = V(v.tensor_tensor(T.o1g[:, 0:8], T.o1f[:, 0:8], T.gm[:, 0:8], OP.mult))
+    wait("v", a)
+    V(v.tensor_reduce(T.msg[:, m0 + 5:m0 + 6], T.o1g[:, 0:8], AxisListType.X, OP.add))
+    wait("v", kaf)
+    a = V(v.transpose(T.at[:, 0:128], T.psf[:, 0:128]))
+    wait("v", kap)
+    V(v.tensor_copy(T.msg[:, m0 + 4:m0 + 5], T.psp[:, 0:1]))
+    wait("v", a)
+    k_msg = V(v.tensor_copy(T.msg[:, m0:m0 + 4], T.at[:, 0:128:32]))
+    wait("g", k_msg)
+    for other in (rank ^ 1, rank ^ 2, rank ^ 3):
+        dst = T.cores[other]
+        rid, pid = topo.addr(dst, core)
+        g.remote_dma(T.msg[:, m0:m0 + 6], T.msg[:, m0:m0 + 6], T.sem["hm"], T.sem["sent"], pid, rid, topo.mask(core, dst))
+        count["sent"] += len(topo.engines(core, dst))
+        count["hm"] = count.get("hm", 0) + len(topo.engines(dst, core))
+    in_msg = ("hm", count["hm"])
+
+    a = V(v.tensor_scalar(T.nb[:, 0:128], T.mk[:, 0:128], -BIG, BIG, OP.mult, OP.add))
+    b2 = V(v.tensor_tensor(T.am0[:, 0:128], T.psf[:, 0:128], T.mk[:, 0:128], OP.mult))
+    wait("v", a, b2)
+    k_am = V(v.tensor_tensor(T.am[:, 0:128], T.am0[:, 0:128], T.nb[:, 0:128], OP.add))
+    k_bas = V(v.tensor_scalar(T.bas[:, 0:8], T.i6[:, 0:8], T.pcf[:, 1:2], 1.0 / 128, OP.add, OP.mult))
+    wait("v", k_i5, k_i7)
+    k_eo = V(v.tensor_copy(T.eoff[:, 0:32], T.i5[:, 0:32]))
+    V(v.tensor_scalar(T.hm[:, 0:32], T.i7[:, 0:32], T.pcf[:, 2:3], None, OP.is_equal))
+    V(v.memset(T.win2[:, 0:512], 0.0))
+    V(v.memset(T.ti2[:, 0:32], 0.0))
+    gc = [T.ga, T.gb, T.gd, T.ge]
+    for c in range(4):
+        far = 0 if c // 2 == rank // 2 else 128
+        V(v.tensor_scalar(T.pos[:, c:c + 1], T.pcf[:, 3:4], float(256 * 512 * c + far), None, OP.add))
+        if c % 2:
+            V(v.tensor_scalar(gc[c][:, 384:385], T.pcf[:, 3:4], -1.0, 127.0, OP.mult, OP.add))
+        else:
+            V(v.tensor_copy(gc[c][:, 384:385], T.pcf[:, 3:4]))
+    wait("v", dw)
+    k_w = V(v.quantize_mx(T.wq[:, 0:256], T.ws[:, 0:256], T.wb[:, 0:1024]))
+
+    wait("t", in1c, in1s)
+    kb = X(t.matmul_mx(T.psf[:, 512:640], T.uq[:, 0:128], T.us[:, 0:128], T.c1[:, 128:256], T.s1[:, 128:256], True, True))
+    wait("v", kb, k_am)
+    a = V(v.tensor_tensor(T.bc[:, 0:128], T.psf[:, 512:640], T.am[:, 0:128], OP.is_ge if rank % 2 else OP.is_gt))
+    wait("v", a)
+    a = V(v.tensor_tensor_scan(T.bs[:, 0:128], T.seg[:, 0:128], T.bc[:, 0:128], 0.0, OP.mult, OP.add))
+    wait("v", a, k_bas)
+    a = V(v.tensor_tensor(T.o2f[:, 0:8], T.bs[:, 15:128:16], T.bas[:, 0:8], OP.add))
+    wait("v", a)
+    k_o2 = V(v.tensor_scalar(T.off2[:, 0:8], T.o2f[:, 0:8], 128.0, None, OP.mult))
+    a2, b2 = pick(T.c2, T.s2, T.c1[:, 0:256], T.s1[:, 0:256], T.off2, (k_o2, in1c), (k_o2, in1s))
+    in2c, in2s = send(T.c2, T.s2, a2, b2, T.cores[rank ^ 2], "h2c", "h2s")
+
+    wait("s", in_msg, k_msg, k_eo)
+    ky = S(s.activation(T.yx[:, 0:512], T.msg[:, 0:32].indirect(T.eoff[:, 0:32]), COPY))
+    wait("v", in_msg)
+    a = V(v.tensor_scalar(T.cp0[:, 0:4], T.msg[:, 5:32:8], 256.0, None, OP.mult))
+    wait("v", a)
+    kcp = V(v.tensor_tensor(T.cp[:, 0:4], T.cp0[:, 0:4], T.pos[:, 0:4], OP.add))
+    wait("v", ky)
+    kfs = V(v.transpose(T.fs[:, 0:512], T.yx[:, 0:512]))
+    wait("s", kcp)
+    for c in range(4):
+        kz = S(s.activation(T.zx[:, 32 * c:32 * c + 32], T.hm[:, 0:32], COPY, scale=T.cp[:, c:c + 1]))
+    wait("v", kfs)
+    pl2 = [None] * 4
+    for c in range(4):
+        sc = T.msg[:, 8 * c + 4:8 * c + 5]
+        if c:
+            k = V(v.tensor_scalar(gc[c][:, 0:128 * c], T.fs[:, 0:128 * c], sc, None, OP.is_ge))
+        if c < 3:
+            k = V(v.tensor_scalar(gc[c][:, 128 * c:384], T.fs[:, 128 * c + 128:512], sc, None, OP.is_gt))
+        pl2[c] = total(gc[c], 0, 385, T.pl2[:, c:c + 1], k)
+    wait("v", kz)
+    a = V(v.transpose(T.zt[:, 0:128], T.zx[:, 0:128]))
+    wait("v", a)
+    for c in range(4):
+        a = V(v.tensor_tensor(T.vals2[:, 16 * c:16 * c + 16], T.zt[:, 32 * c:32 * c + 16], T.zt[:, 32 * c + 16:32 * c + 32], OP.add))
+    k_l2 = invert("2", pl2 + [a], T.pl2, False, T.vals2, True)
+
+    a3, b3 = pick(T.c3, T.s3, T.c2[:, 0:256], T.s2[:, 0:256], T.lst2, (k_l2, in2c), (k_l2, in2s))
+    wait("t", a3, b3, k_w)
+    ko = [X(t.matmul_mx(T.psp[:, 512 * (o + 1):512 * (o + 1) + 128], T.wq[:, 128 * o:128 * o + 128], T.ws[:, 128 * o:128 * o + 128],
+                        T.c3[:, 0:128], T.s3[:, 0:128], True, True)) for o in range(2)]
+    a = V(v.tensor_copy(T.idn[0:32, 0:16], T.tw2[0:32, 0:16]))
+    wait("v", a)
+    V(v.tensor_scalar(T.idr[0:32, 0:16], T.idn[0:32, 0:16], 17, None, OP.arith_shift_right))
+    a = V(v.tensor_scalar(T.idc[0:32, 0:16], T.idn[0:32, 0:16], 8, 511, OP.arith_shift_right, OP.bitwise_and))
+    wait("v", a)
+    V(v.tensor_copy(T.idf[0:32, 0:16], T.idr[0:32, 0:16]))
+    kid = V(v.tensor_copy(T.idf[0:32, 16:32], T.idc[0:32, 0:16]))
+    wait("v", ko[0])
+    ky0 = V(v.tensor_copy(T.yb[:, 0:128], T.psp[:, 512:640]))
+    wait("s", ko[1])
+    ky1 = S(s.activation(T.yb[:, 128:256], T.psp[:, 1024:1152], COPY))
+    wait("y", ky0)
+    d0 = done(y.dma_start(T.y[:, 0:128], T.yb[:, 0:128]), "dy0", 16)
+    wait("s", ky1)
+    d1 = done(s.dma_start(T.y[:, 128:256], T.yb[:, 128:256]), "dy1", 16)
+    wait("y", kid)
+    for row in range(2):
+        d2 = done(y.dma_start(T["id"][row:row + 1, 0:128], T.idf[0:8, 16 * row:16 * row + 16]), "did", 16)
+    wait("g", ("sent", count["sent"]), in1c, in1s, in2c, in2s, in_msg, du, dx[0], dx[1], dx[2], dx[3], dw,
+         ("gc", count["gc"]), ("v", count["v"]), ("s", count["s"]), ("t", count["t"]), d0, d1, d2)

@@ -29,30 +29,32 @@ SCRATCH = {
     "ip": ("sbuf", [128, 32], "int32"), "ipa": ("sbuf", [128, 32], "int32"), "uoff": ("sbuf", [128, 32], "uint16"),
     "it": ("sbuf", [128, 128], "int32"), "ita": ("sbuf", [128, 128], "int32"),
     "mk": ("sbuf", [128, 128], "float32"), "nb": ("sbuf", [128, 128], "float32"),
-    "tri": ("sbuf", [128, 128], "bfloat16"),
     "i3": ("sbuf", [128, 64], "float32"), "vals1": ("sbuf", [128, 64], "float32"),
     "i4": ("sbuf", [128, 128], "float32"), "seg": ("sbuf", [128, 128], "float32"),
-    "i5": ("sbuf", [128, 32], "int32"), "eoff": ("sbuf", [128, 32], "uint16"),
+    "i5": ("sbuf", [128, 16], "int32"), "eoff": ("sbuf", [128, 16], "uint16"),
     "i6": ("sbuf", [128, 8], "float32"), "gm": ("sbuf", [128, 8], "float32"), "bas": ("sbuf", [128, 8], "float32"),
     "i7": ("sbuf", [128, 32], "float32"), "hm": ("sbuf", [128, 32], "float32"),
     "pca": ("sbuf", [128, 4], "int32"), "pcf": ("sbuf", [128, 4], "float32"),
-    "pos": ("sbuf", [128, 4], "float32"),
-    "sf": ("sbuf", [128, 512], "float32"), "sp": ("sbuf", [128, 4], "float32"),
+    "pos": ("sbuf", [128, 2], "float32"),
+    "sf": ("sbuf", [128, 512], "float32"), "sp": ("sbuf", [128, 4], "float32"), "sm": ("sbuf", [128, 512], "float32"),
     "cma": ("sbuf", [128, 644], "float32"), "cmb": ("sbuf", [128, 644], "float32"),
     "cmc": ("sbuf", [128, 644], "float32"), "cmd": ("sbuf", [128, 644], "float32"),
-    "eq": ("sbuf", [128, 512], "bfloat16"), "junk": ("sbuf", [128, 4096], "bfloat16"),
-    "pl1": ("sbuf", [128, 4], "float32"), "pl2": ("sbuf", [128, 4], "float32"),
+    "junk": ("sbuf", [128, 4096], "bfloat16"),
+    "pl1": ("sbuf", [128, 4], "float32"),
     "msg": ("sbuf", [128, 32], "float32"),
     "at": ("sbuf", [128, 128], "float32"), "o1f": ("sbuf", [128, 8], "float32"), "o1g": ("sbuf", [128, 8], "float32"),
     "am0": ("sbuf", [128, 128], "float32"), "am": ("sbuf", [128, 128], "float32"),
     "bc": ("sbuf", [128, 128], "float32"), "bs": ("sbuf", [128, 128], "float32"),
     "o2f": ("sbuf", [128, 8], "float32"), "off2": ("sbuf", [128, 8], "uint16"),
-    "yx": ("sbuf", [128, 512], "float32"), "fs": ("sbuf", [128, 512], "float32"),
-    "ga": ("sbuf", [128, 386], "bfloat16"), "gb": ("sbuf", [128, 386], "bfloat16"),
-    "gd": ("sbuf", [128, 386], "bfloat16"), "ge": ("sbuf", [128, 386], "bfloat16"),
-    "cp0": ("sbuf", [128, 4], "float32"), "cp": ("sbuf", [128, 4], "float32"),
-    "zx": ("sbuf", [128, 128], "float32"), "zt": ("sbuf", [128, 128], "float32"),
-    "vals2": ("sbuf", [128, 64], "float32"),
+    "yx": ("sbuf", [128, 256], "float32"), "fs": ("sbuf", [128, 256], "float32"),
+    "ps": ("sbuf", [128, 2], "float32"), "sel": ("sbuf", [128, 2], "float32"),
+    "ca0": ("sbuf", [128, 130], "bfloat16"), "ca1": ("sbuf", [128, 130], "bfloat16"),
+    "cb0": ("sbuf", [128, 130], "bfloat16"), "cb1": ("sbuf", [128, 130], "bfloat16"),
+    "cx0": ("sbuf", [128, 256], "bfloat16"), "cx1": ("sbuf", [128, 256], "bfloat16"),
+    "acc": ("sbuf", [128, 6], "float32"), "dd": ("sbuf", [128, 2], "float32"),
+    "cp0": ("sbuf", [128, 2], "float32"), "cp1": ("sbuf", [128, 2], "float32"), "cp": ("sbuf", [128, 2], "float32"),
+    "zx": ("sbuf", [128, 64], "float32"), "zt": ("sbuf", [128, 64], "float32"),
+    "vals2": ("sbuf", [128, 32], "float32"),
     "pin": ("sbuf", [32, 8], "int32"), "pia": ("sbuf", [32, 8], "int32"),
     "idn": ("sbuf", [32, 16], "int32"), "idr": ("sbuf", [32, 16], "int32"), "idc": ("sbuf", [32, 16], "int32"),
     "idf": ("sbuf", [32, 32], "float32"),
@@ -67,7 +69,7 @@ for _n in ("1", "2"):
         SCRATCH[_b + _n] = ("sbuf", [32, 32], "float32")
     SCRATCH["lst" + _n] = ("sbuf", [128, 8], "uint16")
 
-SEMAPHORES = ["v", "s", "t", "gc", "du", "dx0", "dx1", "dx2", "dx3", "dw", "dy0", "dy1", "did",
+SEMAPHORES = ["v", "s", "t", "gc", "du", "dx0", "dx1", "dw", "dy0", "dy1", "did",
               "h1c", "h1s", "h2c", "h2s", "hm", "sent"]
 
 
@@ -85,7 +87,10 @@ def rank_program(g, core, T, topo):
         return (sem, count[sem])
 
     def wait(q, *tokens):
+        best = {}
         for sem, n in tokens:
+            best[sem] = max(best.get(sem, 0), n)
+        for sem, n in best.items():
             if waited.get((q, sem), 0) < n:
                 waited[(q, sem)] = n
                 queue[q].wait_ge(T.sem[sem], n)
@@ -94,11 +99,8 @@ def rank_program(g, core, T, topo):
     def S(ins): return done(ins, "s")
     def X(ins): return done(ins, "t")
 
-    du = done(y.dma_start(T.ub[:, 0:4], T.u[:, 0:4]), "du", 16)
-    dx = [None] * 4
-    for d in range(4):
-        q = s if d % 2 else y
-        dx[d] = done(q.dma_start(T.xb[:, 512 * d:512 * d + 512], T.x[:, 512 * d:512 * d + 512]), "dx%d" % d, 16)
+    du = done(s.dma_start(T.ub[:, 0:4], T.u[:, 0:4]), "du", 16)
+    dx = [done(y.dma_start(T.xb[:, 1024 * h:1024 * h + 1024], T.x[:, 1024 * h:1024 * h + 1024]), "dx%d" % h, 16) for h in range(2)]
     dw = done(y.dma_start(T.wb[:, 0:1024], T.w[:, 0:1024]), "dw", 16)
 
     def iota(buf, pattern, base, cm, flt=False):
@@ -106,38 +108,56 @@ def rank_program(g, core, T, topo):
             return done(g.iota(buf, pattern, base, cm, allow_small_or_imprecise_dtypes=True), "gc")
         return done(g.iota(buf, pattern, base, cm), "gc")
     k_ip = iota(T.ip[:, 0:32], [[0, 32]], 0, 1)
-    k_it = iota(T.it[:, 0:128], [[1, 128]], 128, -1)
     k_i3 = iota(T.i3[:, 0:64], [[128, 4], [1, 16]], 0, 0, True)
+    k_it = iota(T.it[:, 0:128], [[1, 128]], 128, -1)
     k_i4 = iota(T.i4[:, 0:128], [[0, 8], [1, 16]], 0, 0, True)
-    k_i5 = iota(T.i5[:, 0:32], [[8, 4], [1, 4], [0, 2]], 0, 0)
     k_i6 = iota(T.i6[:, 0:8], [[16, 8]], 0, 0, True)
+    k_i5 = iota(T.i5[:, 0:16], [[8, 2], [1, 4], [0, 2]], 0, 0)
     k_i7 = iota(T.i7[:, 0:32], [[16, 2], [0, 16]], 0, 0, True)
 
     V(v.memset(T.win1[:, 0:512], 0.0))
     V(v.memset(T.ti1[:, 0:32], 0.0))
     wait("v", k_ip)
     a = V(v.tensor_scalar(T.ipa[:, 0:32], T.ip[:, 0:32], 3, None, OP.bitwise_and))
-    wait("v", a)
-    a = V(v.tensor_copy(T.uoff[:, 0:32], T.ipa[:, 0:32]))
     V(v.tensor_scalar(T.pca[:, 0:1], T.ip[:, 0:1], 112, None, OP.bitwise_and))
     V(v.tensor_scalar(T.pca[:, 1:2], T.ip[:, 0:1], 15, None, OP.bitwise_and))
     V(v.tensor_scalar(T.pca[:, 2:3], T.ip[:, 0:1], 16, None, OP.bitwise_and))
     b = V(v.tensor_copy(T.pca[:, 3:4], T.ip[:, 0:1]))
     wait("v", b)
+    k_uo = V(v.tensor_copy(T.uoff[:, 0:32], T.ipa[:, 0:32]))
     b = V(v.tensor_copy(T.pcf[:, 0:4], T.pca[:, 0:4]))
+    wait("v", b, k_i3)
+    V(v.tensor_scalar(T.vals1[:, 0:64], T.i3[:, 0:64], T.pcf[:, 0:1], None, OP.add))
     wait("v", k_it)
     c = V(v.tensor_scalar(T.ita[:, 0:128], T.it[:, 0:128], 15, None, OP.bitwise_and))
-    V(v.tensor_scalar(T.tri[:, 0:128], T.it[:, 0:128], 128.0, None, OP.is_lt))
-    wait("v", c)
-    V(v.tensor_scalar(T.mk[:, 0:128], T.ita[:, 0:128], 0.0, None, OP.is_equal))
-    wait("v", b, k_i3, k_i4)
-    V(v.tensor_scalar(T.vals1[:, 0:64], T.i3[:, 0:64], T.pcf[:, 0:1], None, OP.add))
-    k_seg = V(v.tensor_scalar(T.seg[:, 0:128], T.i4[:, 0:128], 1.0, None, OP.min))
 
-    wait("v", du, a)
-    a = V(v.tensor_copy(T.ur[:, 0:512], T.ub[:, 0:4].indirect(T.uoff[:, 0:32])))
-    wait("v", a)
+    wait("s", k_uo, du)
+    ks = S(s.activation(T.ur[:, 256:512], T.ub[:, 0:4].indirect(T.uoff[:, 16:32]), COPY))
+    wait("v", du, k_uo)
+    a = V(v.tensor_copy(T.ur[:, 0:256], T.ub[:, 0:4].indirect(T.uoff[:, 0:16])))
+    wait("v", a, ks)
     k_u = V(v.quantize_mx(T.uq[:, 0:128], T.us[:, 0:128], T.ur[:, 0:512]))
+    wait("v", c, k_i4)
+    V(v.tensor_scalar(T.mk[:, 0:128], T.ita[:, 0:128], 0.0, None, OP.is_equal))
+    V(v.tensor_scalar(T.seg[:, 0:128], T.i4[:, 0:128], 1.0, None, OP.min))
+
+    kp, kf = [None] * 4, [None] * 2
+    for h in range(2):
+        e = slice(256 * h, 256 * h + 256)
+        wait("v", dx[h])
+        kq = V(v.quantize_mx(T.xq[:, e], T.xs[:, e], T.xb[:, 1024 * h:1024 * h + 1024]))
+        wait("t", k_u, kq)
+        kf[h] = X(t.matmul_mx(T.psf[:, 512 * h:512 * h + 256], T.uq[:, 0:128], T.us[:, 0:128], T.xq[:, e], T.xs[:, e], True, True))
+        for c in (2 * h, 2 * h + 1):
+            e2 = slice(128 * c, 128 * c + 128)
+            kp[c] = X(t.matmul_mx(T.psp[:, 512 * c:512 * c + 128], T.xq[:, e2], T.xs[:, e2], T.uq[:, 0:128], T.us[:, 0:128], True, True))
+        wait("s", kf[h])
+        kf[h] = S(s.activation(T.sf[:, e], T.psf[:, 512 * h:512 * h + 256], COPY))
+    km = [None] * 4
+    for c in range(4):
+        wait("g", kf[c // 2])
+        e2 = slice(128 * c, 128 * c + 128)
+        km[c] = done(g.affine_select(T.sm[:, e2], T.sf[:, e2], [[-1, 128]], OP.is_gt, BIG, 0, 1), "gc")
 
     cm = [T.cma, T.cmb, T.cmc, T.cmd]
     jk = [0]
@@ -149,50 +169,46 @@ def rank_program(g, core, T, topo):
         jk[0] = jk[0] + n if jk[0] + n + 700 <= 4096 else 0
         return r
 
-    def blk(d): return slice(128 * d, 128 * d + 128) if d < 3 else slice(513, 641)
-    early = [None] * 4
+    def cmp(out, src, col, op):
+        return V(v.tensor_scalar(out, src, col, None, op))
+    sp = [T.sp[:, c:c + 1] for c in range(4)]
+    sf, sm = T.sf, T.sm
+    wait("v", kp[1])
+    V(v.tensor_copy(sp[0], T.psp[:, 0:1]))
+    a = V(v.tensor_copy(sp[1], T.psp[:, 512:513]))
+    wait("v", a, kf[0])
+    cmp(cm[0][:, 0:256], sf[:, 0:256], sp[0], OP.is_gt)
+    cmp(cm[1][:, 0:128], sf[:, 0:128], sp[1], OP.is_ge)
+    cmp(cm[1][:, 128:256], sf[:, 128:256], sp[1], OP.is_gt)
+    wait("v", km[0])
+    e0 = cmp(cm[0][:, 256:384], sm[:, 0:128], sp[0], OP.is_equal)
+    wait("v", km[1])
+    e1 = cmp(cm[1][:, 256:384], sm[:, 128:256], sp[1], OP.is_equal)
+    e0 = total(cm[0], 0, 384, cm[0][:, 384:385], e0)
+    e1 = total(cm[1], 0, 384, cm[1][:, 384:385], e1)
+    wait("v", kp[3])
+    V(v.tensor_copy(sp[2], T.psp[:, 1024:1025]))
+    a = V(v.tensor_copy(sp[3], T.psp[:, 1536:1537]))
+    wait("v", a, kf[1])
+    cmp(cm[2][:, 0:256], sf[:, 0:256], sp[2], OP.is_ge)
+    e2 = cmp(cm[2][:, 256:512], sf[:, 256:512], sp[2], OP.is_gt)
+    e2 = total(cm[2], 0, 512, cm[2][:, 640:641], e2)
+    cmp(cm[3][:, 0:384], sf[:, 0:384], sp[3], OP.is_ge)
+    e3 = cmp(cm[3][:, 384:512], sf[:, 384:512], sp[3], OP.is_gt)
+    e3 = total(cm[3], 0, 512, cm[3][:, 640:641], e3)
     pl = [None] * 4
-    for d in range(4):
-        e = slice(128 * d, 128 * d + 128)
-        wait("v", dx[d])
-        kq = V(v.quantize_mx(T.xq[:, e], T.xs[:, e], T.xb[:, 512 * d:512 * d + 512]))
-        wait("t", k_u, kq)
-        kf = X(t.matmul_mx(T.psf[:, 512 * d:512 * d + 128], T.uq[:, 0:128], T.us[:, 0:128], T.xq[:, e], T.xs[:, e], True, True))
-        kp = X(t.matmul_mx(T.psp[:, 512 * d:512 * d + 128], T.xq[:, e], T.xs[:, e], T.uq[:, 0:128], T.us[:, 0:128], True, True))
-        wait("s", kf)
-        kf = S(s.activation(T.sf[:, e], T.psf[:, 512 * d:512 * d + 128], COPY))
-        wait("v", kp)
-        kp = V(v.tensor_copy(T.sp[:, d:d + 1], T.psp[:, 512 * d:512 * d + 1]))
-        wait("v", kp, kf)
-        me = T.sp[:, d:d + 1]
-        if d:
-            kge = V(v.tensor_scalar(cm[d][:, 0:128 * d], T.sf[:, 0:128 * d], me, None, OP.is_ge))
-        if d == 3:
-            early[3] = total(cm[3], 0, 384, cm[3][:, 512:513], kge)
-        low = [V(v.tensor_scalar(cm[c][:, blk(d)], T.sf[:, e], T.sp[:, c:c + 1], None, OP.is_gt)) for c in range(d)]
-        if d == 3:
-            for c in range(3):
-                pl[c] = total(cm[c], 512, 641, T.pl1[:, c:c + 1], low[c], early[c])
-        keq = V(v.tensor_scalar(T.eq[:, e], T.sf[:, e], me, None, OP.is_equal))
-        V(v.tensor_scalar(cm[d][:, blk(d)], T.sf[:, e], me, None, OP.is_gt))
-        wait("v", keq)
-        kown = V(v.tensor_tensor(cm[d][:, 384:512], T.eq[:, e], T.tri[:, 0:128], OP.mult))
-        if d == 2:
-            for c in range(3):
-                early[c] = total(cm[c], 0, 512, cm[c][:, 512:513], kown)
-        if d == 3:
-            pl[3] = total(cm[3], 384, 641, T.pl1[:, 3:4], kown, early[3])
+    for c, e in ((0, e0), (1, e1)):
+        a = cmp(cm[c][:, 385:641], sf[:, 256:512], sp[c], OP.is_gt)
+        pl[c] = total(cm[c], 384, 641, T.pl1[:, c:c + 1], a, e)
+    for c, e in ((2, e2), (3, e3)):
+        wait("v", km[c])
+        a = cmp(cm[c][:, 512:640], sm[:, 128 * c:128 * c + 128], sp[c], OP.is_equal)
+        pl[c] = total(cm[c], 512, 641, T.pl1[:, c:c + 1], a, e)
 
-    def invert(n, places, plbuf, flip, vals, low8):
+    def invert(n, ready, cols, vals, lo, low8):
         W = lambda b: T[b + n]
-        wait("v", *places)
-        if flip:
-            a = V(v.tensor_scalar(W("pu")[:, 0:4], plbuf[:, 0:4], -1.0, 511.0, OP.mult, OP.add))
-        else:
-            a = V(v.tensor_copy(W("pu")[:, 0:4], plbuf[:, 0:4]))
-        lo = 384 if flip else 0
-        wait("v", a)
-        a = V(v.tensor_copy(W("win")[:, 0:512].indirect(W("pu")[:, 0:4]), vals[:, 0:64]))
+        wait("v", *ready)
+        a = V(v.tensor_copy(W("win")[:, 0:512].indirect(W("pu")[:, 0:cols]), vals[:, 0:16 * cols]))
         wait("v", a)
         a = V(v.tensor_tensor(W("wm")[:, 0:128], W("win")[:, lo:lo + 128], T.mk[:, 0:128], OP.mult))
         wait("v", a)
@@ -240,7 +256,13 @@ def rank_program(g, core, T, topo):
             count["sent"] = count.get("sent", 0) + n
         return (sem_c, n), (sem_s, n)
 
-    k_l1 = invert("1", pl, T.pl1, rank % 2 == 1, T.vals1, False)
+    odd = rank % 2
+    wait("v", *pl)
+    if odd:
+        a = V(v.tensor_scalar(T.pu1[:, 0:4], T.pl1[:, 0:4], -1.0, 511.0, OP.mult, OP.add))
+    else:
+        a = V(v.tensor_copy(T.pu1[:, 0:4], T.pl1[:, 0:4]))
+    k_l1 = invert("1", (a,), 4, T.vals1, 384 if odd else 0, False)
     a1, b1 = pick(T.c1, T.s1, T.xq[:, 0:512], T.xs[:, 0:512], T.lst1, (k_l1,), (k_l1,))
     mate = T.cores[rank ^ 1]
     in1c, in1s = send(T.c1, T.s1, a1, b1, mate, "h1c", "h1s")
@@ -249,27 +271,31 @@ def rank_program(g, core, T, topo):
     wait("t", a1, b1)
     kaf = X(t.matmul_mx(T.psf[:, 0:128], T.uq[:, 0:128], T.us[:, 0:128], T.c1[:, 0:128], T.s1[:, 0:128], True, True))
     kap = X(t.matmul_mx(T.psp[:, 0:128], T.c1[:, 0:128], T.s1[:, 0:128], T.uq[:, 0:128], T.us[:, 0:128], True, True))
-    wait("v", k_l1, k_i6, b)
+    wait("v", k_i6)
     V(v.tensor_scalar(T.gm[:, 0:8], T.i6[:, 0:8], T.pcf[:, 0:1], None, OP.is_equal))
     a = V(v.tensor_copy(T.o1f[:, 0:8], T.lst1[:, 0:8]))
     wait("v", a)
     a = V(v.tensor_tensor(T.o1g[:, 0:8], T.o1f[:, 0:8], T.gm[:, 0:8], OP.mult))
-    wait("v", a)
+    wait("v", a, kaf)
+    a2 = V(v.transpose(T.at[:, 0:128], T.psf[:, 0:128]))
     V(v.tensor_reduce(T.msg[:, m0 + 5:m0 + 6], T.o1g[:, 0:8], AxisListType.X, OP.add))
-    wait("v", kaf)
-    a = V(v.transpose(T.at[:, 0:128], T.psf[:, 0:128]))
     wait("v", kap)
     V(v.tensor_copy(T.msg[:, m0 + 4:m0 + 5], T.psp[:, 0:1]))
-    wait("v", a)
+    wait("v", a2)
     k_msg = V(v.tensor_copy(T.msg[:, m0:m0 + 4], T.at[:, 0:128:32]))
     wait("g", k_msg)
+    ids, m = [], 0xFFFF
     for other in (rank ^ 1, rank ^ 2, rank ^ 3):
         dst = T.cores[other]
         rid, pid = topo.addr(dst, core)
-        g.remote_dma(T.msg[:, m0:m0 + 6], T.msg[:, m0:m0 + 6], T.sem["hm"], T.sem["sent"], pid, rid, topo.mask(core, dst))
-        count["sent"] += len(topo.engines(core, dst))
-        count["hm"] = count.get("hm", 0) + len(topo.engines(dst, core))
-    in_msg = ("hm", count["hm"])
+        ids.append(DstId(rid=rid, pnc=pid))
+        m &= topo.mask(core, dst)
+    n = bin(m).count("1")
+    view = T.msg[:, m0:m0 + 6]
+    g.remote_dma_fused([RemoteDMATransfer(dst_ids=ids, dma_engine_mask=m, remote_sem=T.sem["hm"], srcs=[view], dsts=[view] * 3)],
+                       local_sem=T.sem["sent"])
+    count["sent"] += n
+    in_msg = ("hm", 3 * n)
 
     a = V(v.tensor_scalar(T.nb[:, 0:128], T.mk[:, 0:128], -BIG, BIG, OP.mult, OP.add))
     b2 = V(v.tensor_tensor(T.am0[:, 0:128], T.psf[:, 0:128], T.mk[:, 0:128], OP.mult))
@@ -277,25 +303,24 @@ def rank_program(g, core, T, topo):
     k_am = V(v.tensor_tensor(T.am[:, 0:128], T.am0[:, 0:128], T.nb[:, 0:128], OP.add))
     k_bas = V(v.tensor_scalar(T.bas[:, 0:8], T.i6[:, 0:8], T.pcf[:, 1:2], 1.0 / 128, OP.add, OP.mult))
     wait("v", k_i5, k_i7)
-    k_eo = V(v.tensor_copy(T.eoff[:, 0:32], T.i5[:, 0:32]))
+    k_eo = V(v.tensor_copy(T.eoff[:, 0:16], T.i5[:, 0:16]))
     V(v.tensor_scalar(T.hm[:, 0:32], T.i7[:, 0:32], T.pcf[:, 2:3], None, OP.is_equal))
     V(v.memset(T.win2[:, 0:512], 0.0))
     V(v.memset(T.ti2[:, 0:32], 0.0))
-    gc = [T.ga, T.gb, T.gd, T.ge]
-    for c in range(4):
-        far = 0 if c // 2 == rank // 2 else 128
-        V(v.tensor_scalar(T.pos[:, c:c + 1], T.pcf[:, 3:4], float(256 * 512 * c + far), None, OP.add))
-        if c % 2:
-            V(v.tensor_scalar(gc[c][:, 384:385], T.pcf[:, 3:4], -1.0, 127.0, OP.mult, OP.add))
-        else:
-            V(v.tensor_copy(gc[c][:, 384:385], T.pcf[:, 3:4]))
+    pair = rank // 2
+    ca, cb, cx = (T.ca0, T.ca1), (T.cb0, T.cb1), (T.cx0, T.cx1)
+    for j in range(2):
+        V(v.tensor_scalar(T.pos[:, j:j + 1], T.pcf[:, 3:4], float(256 * 1024 * (pair ^ j) + 128 * j), None, OP.add))
+        V(v.tensor_copy(ca[j][:, 128:129], T.pcf[:, 3:4]))
+        V(v.tensor_scalar(cb[j][:, 128:129], T.pcf[:, 3:4], -1.0, 127.0, OP.mult, OP.add))
     wait("v", dw)
     k_w = V(v.quantize_mx(T.wq[:, 0:256], T.ws[:, 0:256], T.wb[:, 0:1024]))
 
     wait("t", in1c, in1s)
     kb = X(t.matmul_mx(T.psf[:, 512:640], T.uq[:, 0:128], T.us[:, 0:128], T.c1[:, 128:256], T.s1[:, 128:256], True, True))
+    kbp = X(t.matmul_mx(T.psp[:, 512:640], T.c1[:, 128:256], T.s1[:, 128:256], T.uq[:, 0:128], T.us[:, 0:128], True, True))
     wait("v", kb, k_am)
-    a = V(v.tensor_tensor(T.bc[:, 0:128], T.psf[:, 512:640], T.am[:, 0:128], OP.is_ge if rank % 2 else OP.is_gt))
+    a = V(v.tensor_tensor(T.bc[:, 0:128], T.psf[:, 512:640], T.am[:, 0:128], OP.is_ge if odd else OP.is_gt))
     wait("v", a)
     a = V(v.tensor_tensor_scan(T.bs[:, 0:128], T.seg[:, 0:128], T.bc[:, 0:128], 0.0, OP.mult, OP.add))
     wait("v", a, k_bas)
@@ -305,36 +330,66 @@ def rank_program(g, core, T, topo):
     a2, b2 = pick(T.c2, T.s2, T.c1[:, 0:256], T.s1[:, 0:256], T.off2, (k_o2, in1c), (k_o2, in1s))
     in2c, in2s = send(T.c2, T.s2, a2, b2, T.cores[rank ^ 2], "h2c", "h2s")
 
-    wait("s", in_msg, k_msg, k_eo)
-    ky = S(s.activation(T.yx[:, 0:512], T.msg[:, 0:32].indirect(T.eoff[:, 0:32]), COPY))
+    j1 = pair ^ 1
+    wait("s", in_msg, k_eo)
+    ky = S(s.activation(T.yx[:, 0:256], T.msg[:, 16 * j1:16 * j1 + 16].indirect(T.eoff[:, 0:16]), COPY))
+    ps, sel = [T.ps[:, j:j + 1] for j in range(2)], [T.sel[:, j:j + 1] for j in range(2)]
+    acc = [T.acc[:, j:j + 1] for j in range(6)]
+    mine, his = T.msg[:, m0 + 4:m0 + 5], T.psp[:, 512:513]
+    fr = (T.psf[:, 512:640], T.psf[:, 0:128]) if odd else (T.psf[:, 0:128], T.psf[:, 512:640])
+    wait("v", kbp)
+    V(v.tensor_tensor(ps[0], his, mine, OP.max))
+    a = V(v.tensor_tensor(sel[0], his, mine, OP.is_lt if odd else OP.is_gt))
+    wait("v", a)
+    a = cmp(ca[0][:, 0:128], fr[1], ps[0], OP.is_gt)
+    b = cmp(cb[0][:, 0:128], fr[0], ps[0], OP.is_ge)
+    ka = [None] * 6
+    ka[0] = total(ca[0], 0, 129, acc[0], a)
+    ka[1] = total(cb[0], 0, 129, acc[1], b)
+    col = lambda c, w: T.msg[:, 8 * c + w:8 * c + w + 1]
     wait("v", in_msg)
-    a = V(v.tensor_scalar(T.cp0[:, 0:4], T.msg[:, 5:32:8], 256.0, None, OP.mult))
-    wait("v", a)
-    kcp = V(v.tensor_tensor(T.cp[:, 0:4], T.cp0[:, 0:4], T.pos[:, 0:4], OP.add))
+    V(v.tensor_tensor(ps[1], col(2 * j1, 4), col(2 * j1 + 1, 4), OP.max))
+    a = V(v.tensor_tensor(sel[1], col(2 * j1 + 1, 4), col(2 * j1, 4), OP.is_gt))
+    for j in range(2):
+        b = V(v.tensor_scalar(T.cp0[:, j:j + 1], col(2 * (pair ^ j) + 1, 5), col(2 * (pair ^ j), 5), 512.0, OP.subtract, OP.add))
+    wait("v", a, b)
+    for f in range(2):
+        k = cmp(cx[1][:, 128 * f:128 * f + 128], fr[f], ps[1], OP.is_ge if pair == 0 else OP.is_gt)
+    ka[5] = total(cx[1], 0, 256, acc[5], k)
+    for j in range(2):
+        b = V(v.tensor_scalar(T.cp1[:, j:j + 1], T.cp0[:, j:j + 1], sel[j], col(2 * (pair ^ j), 5), OP.mult, OP.add))
+    wait("v", b)
+    for j in range(2):
+        kcp = V(v.tensor_scalar(T.cp[:, j:j + 1], T.cp1[:, j:j + 1], 256.0, T.pos[:, j:j + 1], OP.mult, OP.add))
     wait("v", ky)
-    kfs = V(v.transpose(T.fs[:, 0:512], T.yx[:, 0:512]))
+    k = V(v.transpose(T.fs[:, 0:256], T.yx[:, 0:256]))
+    wait("v", k)
+    k = cmp(cx[0][:, 0:256], T.fs[:, 0:256], ps[0], OP.is_ge if pair == 1 else OP.is_gt)
+    a = cmp(ca[1][:, 0:128], T.fs[:, 128:256], ps[1], OP.is_gt)
+    b = cmp(cb[1][:, 0:128], T.fs[:, 0:128], ps[1], OP.is_ge)
     wait("s", kcp)
-    for c in range(4):
-        kz = S(s.activation(T.zx[:, 32 * c:32 * c + 32], T.hm[:, 0:32], COPY, scale=T.cp[:, c:c + 1]))
-    wait("v", kfs)
-    pl2 = [None] * 4
-    for c in range(4):
-        sc = T.msg[:, 8 * c + 4:8 * c + 5]
-        if c:
-            k = V(v.tensor_scalar(gc[c][:, 0:128 * c], T.fs[:, 0:128 * c], sc, None, OP.is_ge))
-        if c < 3:
-            k = V(v.tensor_scalar(gc[c][:, 128 * c:384], T.fs[:, 128 * c + 128:512], sc, None, OP.is_gt))
-        pl2[c] = total(gc[c], 0, 385, T.pl2[:, c:c + 1], k)
+    for j in range(2):
+        kz = S(s.activation(T.zx[:, 32 * j:32 * j + 32], T.hm[:, 0:32], COPY, scale=T.cp[:, j:j + 1]))
+    ka[4] = total(cx[0], 0, 256, acc[4], k)
+    ka[2] = total(ca[1], 0, 129, acc[2], a)
+    ka[3] = total(cb[1], 0, 129, acc[3], b)
     wait("v", kz)
-    a = V(v.transpose(T.zt[:, 0:128], T.zx[:, 0:128]))
+    a = V(v.transpose(T.zt[:, 0:64], T.zx[:, 0:64]))
+    wait("v", ka[0], ka[1])
+    V(v.tensor_scalar(T.dd[:, 0:1], acc[1], acc[0], sel[0], OP.subtract, OP.mult))
     wait("v", a)
-    for c in range(4):
-        a = V(v.tensor_tensor(T.vals2[:, 16 * c:16 * c + 16], T.zt[:, 32 * c:32 * c + 16], T.zt[:, 32 * c + 16:32 * c + 32], OP.add))
-    k_l2 = invert("2", pl2 + [a], T.pl2, False, T.vals2, True)
+    for j in range(2):
+        kv = V(v.tensor_tensor(T.vals2[:, 16 * j:16 * j + 16], T.zt[:, 32 * j:32 * j + 16], T.zt[:, 32 * j + 16:32 * j + 32], OP.add))
+    wait("v", ka[2], ka[3])
+    a = V(v.tensor_scalar(T.dd[:, 1:2], acc[3], acc[2], sel[1], OP.subtract, OP.mult))
+    wait("v", a, ka[4], ka[5])
+    for j in range(2):
+        kv = V(v.tensor_scalar(T.pu2[:, j:j + 1], T.dd[:, j:j + 1], acc[2 * j], acc[4 + j], OP.add, OP.add))
+    k_l2 = invert("2", (kv,), 2, T.vals2, 0, True)
 
     a3, b3 = pick(T.c3, T.s3, T.c2[:, 0:256], T.s2[:, 0:256], T.lst2, (k_l2, in2c), (k_l2, in2s))
     wait("t", a3, b3, k_w)
-    ko = [X(t.matmul_mx(T.psp[:, 512 * (o + 1):512 * (o + 1) + 128], T.wq[:, 128 * o:128 * o + 128], T.ws[:, 128 * o:128 * o + 128],
+    ko = [X(t.matmul_mx(T.psp[:, 512 * (o + 2):512 * (o + 2) + 128], T.wq[:, 128 * o:128 * o + 128], T.ws[:, 128 * o:128 * o + 128],
                         T.c3[:, 0:128], T.s3[:, 0:128], True, True)) for o in range(2)]
     a = V(v.tensor_copy(T.idn[0:32, 0:16], T.tw2[0:32, 0:16]))
     wait("v", a)
@@ -344,9 +399,9 @@ def rank_program(g, core, T, topo):
     V(v.tensor_copy(T.idf[0:32, 0:16], T.idr[0:32, 0:16]))
     kid = V(v.tensor_copy(T.idf[0:32, 16:32], T.idc[0:32, 0:16]))
     wait("v", ko[0])
-    ky0 = V(v.tensor_copy(T.yb[:, 0:128], T.psp[:, 512:640]))
+    ky0 = V(v.tensor_copy(T.yb[:, 0:128], T.psp[:, 1024:1152]))
     wait("s", ko[1])
-    ky1 = S(s.activation(T.yb[:, 128:256], T.psp[:, 1024:1152], COPY))
+    ky1 = S(s.activation(T.yb[:, 128:256], T.psp[:, 1536:1664], COPY))
     wait("y", ky0)
     d0 = done(y.dma_start(T.y[:, 0:128], T.yb[:, 0:128]), "dy0", 16)
     wait("s", ky1)
@@ -354,5 +409,5 @@ def rank_program(g, core, T, topo):
     wait("y", kid)
     for row in range(2):
         d2 = done(y.dma_start(T["id"][row:row + 1, 0:128], T.idf[0:8, 16 * row:16 * row + 16]), "did", 16)
-    wait("g", ("sent", count["sent"]), in1c, in1s, in2c, in2s, in_msg, du, dx[0], dx[1], dx[2], dx[3], dw,
+    wait("g", ("sent", count["sent"]), in1c, in1s, in2c, in2s, in_msg, du, dx[0], dx[1], dw,
          ("gc", count["gc"]), ("v", count["v"]), ("s", count["s"]), ("t", count["t"]), d0, d1, d2)

@@ -5,6 +5,8 @@ OP = AluOpType
 COPY = ActivationFunctionType.Copy
 K = 128
 BIG = 1e29
+LIFT = 256.0
+GID = 4096
 
 SCRATCH = {
     "ub": ("sbuf", [128, 16], "bfloat16"),
@@ -29,23 +31,23 @@ SCRATCH = {
     "ip": ("sbuf", [128, 32], "int32"), "ipa": ("sbuf", [128, 32], "int32"), "uoff": ("sbuf", [128, 32], "uint16"),
     "it": ("sbuf", [128, 128], "int32"), "ita": ("sbuf", [128, 128], "int32"),
     "mk": ("sbuf", [128, 128], "float32"), "nb": ("sbuf", [128, 128], "float32"),
+    "ch0": ("sbuf", [128, 128], "float32"), "ch1": ("sbuf", [128, 128], "float32"), "ch": ("sbuf", [128, 128], "float32"),
     "i3": ("sbuf", [128, 64], "float32"), "vals1": ("sbuf", [128, 64], "float32"),
-    "i4": ("sbuf", [128, 128], "float32"), "seg": ("sbuf", [128, 128], "float32"),
     "i5": ("sbuf", [128, 16], "int32"), "eoff": ("sbuf", [128, 16], "uint16"),
-    "i6": ("sbuf", [128, 8], "float32"), "gm": ("sbuf", [128, 8], "float32"), "bas": ("sbuf", [128, 8], "float32"),
+    "i6": ("sbuf", [128, 8], "float32"), "gm": ("sbuf", [128, 8], "float32"), "hs": ("sbuf", [128, 128], "float32"),
     "i7": ("sbuf", [128, 32], "float32"), "hm": ("sbuf", [128, 32], "float32"),
-    "pca": ("sbuf", [128, 4], "int32"), "pcf": ("sbuf", [128, 4], "float32"),
+    "pca": ("sbuf", [128, 4], "int32"), "pcf": ("sbuf", [128, 4], "float32"), "pcq": ("sbuf", [128, 2], "float32"),
     "pos": ("sbuf", [128, 2], "float32"),
     "sf": ("sbuf", [128, 512], "float32"), "sp": ("sbuf", [128, 4], "float32"), "sm": ("sbuf", [128, 512], "float32"),
     "cma": ("sbuf", [128, 644], "float32"), "cmb": ("sbuf", [128, 644], "float32"),
     "cmc": ("sbuf", [128, 644], "float32"), "cmd": ("sbuf", [128, 644], "float32"),
     "junk": ("sbuf", [128, 4096], "bfloat16"),
-    "pl1": ("sbuf", [128, 4], "float32"),
+    "pl1": ("sbuf", [128, 4], "float32"), "pl3": ("sbuf", [128, 1], "float32"),
     "msg": ("sbuf", [128, 32], "float32"),
     "at": ("sbuf", [128, 128], "float32"), "o1f": ("sbuf", [128, 8], "float32"), "o1g": ("sbuf", [128, 8], "float32"),
     "am0": ("sbuf", [128, 128], "float32"), "am": ("sbuf", [128, 128], "float32"),
     "bc": ("sbuf", [128, 128], "float32"), "bs": ("sbuf", [128, 128], "float32"),
-    "o2f": ("sbuf", [128, 8], "float32"), "off2": ("sbuf", [128, 8], "uint16"),
+    "off2": ("sbuf", [128, 8], "uint16"),
     "yx": ("sbuf", [128, 256], "float32"), "fs": ("sbuf", [128, 256], "float32"),
     "ps": ("sbuf", [128, 2], "float32"), "sel": ("sbuf", [128, 2], "float32"),
     "ca0": ("sbuf", [128, 130], "bfloat16"), "ca1": ("sbuf", [128, 130], "bfloat16"),
@@ -55,22 +57,20 @@ SCRATCH = {
     "cp0": ("sbuf", [128, 2], "float32"), "cp1": ("sbuf", [128, 2], "float32"), "cp": ("sbuf", [128, 2], "float32"),
     "zx": ("sbuf", [128, 64], "float32"), "zt": ("sbuf", [128, 64], "float32"),
     "vals2": ("sbuf", [128, 32], "float32"),
-    "pin": ("sbuf", [32, 8], "int32"), "pia": ("sbuf", [32, 8], "int32"),
     "idn": ("sbuf", [32, 16], "int32"), "idr": ("sbuf", [32, 16], "int32"), "idc": ("sbuf", [32, 16], "int32"),
     "idf": ("sbuf", [32, 32], "float32"),
 }
 for _n in ("1", "2"):
     SCRATCH["pu" + _n] = ("sbuf", [128, 4], "uint16")
     SCRATCH["win" + _n] = ("sbuf", [128, 512], "float32")
-    SCRATCH["wm" + _n] = ("sbuf", [128, 128], "float32")
     SCRATCH["sc" + _n] = ("sbuf", [128, 128], "float32")
     SCRATCH["qa" + _n] = ("sbuf", [64, 8], "float32")
     for _b in ("ti", "to", "tw", "tb"):
         SCRATCH[_b + _n] = ("sbuf", [32, 32], "float32")
     SCRATCH["lst" + _n] = ("sbuf", [128, 8], "uint16")
 
-SEMAPHORES = ["v", "s", "t", "gc", "du", "dx0", "dx1", "dw", "dy0", "dy1", "did",
-              "h1c", "h1s", "h2c", "h2s", "hm", "sent"]
+SEMAPHORES = ["v", "s", "t", "gc", "du", "dx0", "dx1", "dx2", "dx3", "dw", "dy0", "dy1", "did",
+              "h1c", "h1s", "h2c", "h2s", "hm", "hp", "sent"]
 
 
 def rank_program(g, core, T, topo):
@@ -80,6 +80,7 @@ def rank_program(g, core, T, topo):
     v, s, t, y = g.vector, g.scalar, g.tensor, g.sync
     queue = {"g": g, "v": v, "s": s, "t": t, "y": y}
     count, waited = {}, {}
+    odd, pair = rank % 2, rank // 2
 
     def done(ins, sem, n=1):
         ins.then_inc(T.sem[sem], n)
@@ -100,7 +101,7 @@ def rank_program(g, core, T, topo):
     def X(ins): return done(ins, "t")
 
     du = done(s.dma_start(T.ub[:, 0:4], T.u[:, 0:4]), "du", 16)
-    dx = [done(y.dma_start(T.xb[:, 1024 * h:1024 * h + 1024], T.x[:, 1024 * h:1024 * h + 1024]), "dx%d" % h, 16) for h in range(2)]
+    dx = [done(y.dma_start(T.xb[:, 512 * d:512 * d + 512], T.x[:, 512 * d:512 * d + 512]), "dx%d" % d, 16) for d in range(4)]
     dw = done(y.dma_start(T.wb[:, 0:1024], T.w[:, 0:1024]), "dw", 16)
 
     def iota(buf, pattern, base, cm, flt=False):
@@ -110,13 +111,13 @@ def rank_program(g, core, T, topo):
     k_ip = iota(T.ip[:, 0:32], [[0, 32]], 0, 1)
     k_i3 = iota(T.i3[:, 0:64], [[128, 4], [1, 16]], 0, 0, True)
     k_it = iota(T.it[:, 0:128], [[1, 128]], 128, -1)
-    k_i4 = iota(T.i4[:, 0:128], [[0, 8], [1, 16]], 0, 0, True)
     k_i6 = iota(T.i6[:, 0:8], [[16, 8]], 0, 0, True)
     k_i5 = iota(T.i5[:, 0:16], [[8, 2], [1, 4], [0, 2]], 0, 0)
     k_i7 = iota(T.i7[:, 0:32], [[16, 2], [0, 16]], 0, 0, True)
 
     V(v.memset(T.win1[:, 0:512], 0.0))
     V(v.memset(T.ti1[:, 0:32], 0.0))
+    V(v.memset(T.cmd[:, 640:641], -511.0 if odd else 0.0))
     wait("v", k_ip)
     a = V(v.tensor_scalar(T.ipa[:, 0:32], T.ip[:, 0:32], 3, None, OP.bitwise_and))
     V(v.tensor_scalar(T.pca[:, 0:1], T.ip[:, 0:1], 112, None, OP.bitwise_and))
@@ -127,9 +128,13 @@ def rank_program(g, core, T, topo):
     k_uo = V(v.tensor_copy(T.uoff[:, 0:32], T.ipa[:, 0:32]))
     b = V(v.tensor_copy(T.pcf[:, 0:4], T.pca[:, 0:4]))
     wait("v", b, k_i3)
-    V(v.tensor_scalar(T.vals1[:, 0:64], T.i3[:, 0:64], T.pcf[:, 0:1], None, OP.add))
+    V(v.tensor_scalar(T.vals1[:, 0:64], T.i3[:, 0:64], T.pcf[:, 0:1], 0.5, OP.add, OP.mult))
+    V(v.tensor_scalar(T.pcq[:, 0:1], T.pcf[:, 1:2], 15.0, -8 * LIFT, OP.is_lt, OP.mult))
+    V(v.tensor_scalar(T.pcq[:, 1:2], T.pcf[:, 1:2], 128.0, None, OP.add))
     wait("v", k_it)
-    c = V(v.tensor_scalar(T.ita[:, 0:128], T.it[:, 0:128], 15, None, OP.bitwise_and))
+    a = V(v.tensor_scalar(T.ita[:, 0:128], T.it[:, 0:128], 15, None, OP.bitwise_and))
+    wait("v", a)
+    V(v.tensor_scalar(T.ch0[:, 0:128], T.ita[:, 0:128], 0.0, -65536.0, OP.is_equal, OP.mult))
 
     wait("s", k_uo, du)
     ks = S(s.activation(T.ur[:, 256:512], T.ub[:, 0:4].indirect(T.uoff[:, 16:32]), COPY))
@@ -137,27 +142,39 @@ def rank_program(g, core, T, topo):
     a = V(v.tensor_copy(T.ur[:, 0:256], T.ub[:, 0:4].indirect(T.uoff[:, 0:16])))
     wait("v", a, ks)
     k_u = V(v.quantize_mx(T.uq[:, 0:128], T.us[:, 0:128], T.ur[:, 0:512]))
-    wait("v", c, k_i4)
-    V(v.tensor_scalar(T.mk[:, 0:128], T.ita[:, 0:128], 0.0, None, OP.is_equal))
-    V(v.tensor_scalar(T.seg[:, 0:128], T.i4[:, 0:128], 1.0, None, OP.min))
 
+    kq = [None] * 4
+    for d in range(4):
+        e = slice(128 * d, 128 * d + 128)
+        wait("v", dx[d])
+        kq[d] = V(v.quantize_mx(T.xq[:, e], T.xs[:, e], T.xb[:, 512 * d:512 * d + 512]))
+        if d == 0:
+            k_ch = V(v.tensor_scalar(T.ch1[:, 0:128], T.ita[:, 0:128], 1.0, LIFT, OP.is_equal, OP.mult))
+        if d == 1:
+            wait("v", k_ch)
+            k_ch = V(v.tensor_tensor(T.ch[:, 0:128], T.ch0[:, 0:128], T.ch1[:, 0:128], OP.add))
     kp, kf = [None] * 4, [None] * 2
-    for h in range(2):
+
+    def scores_down(c):
+        e = slice(128 * c, 128 * c + 128)
+        wait("t", k_u, kq[c])
+        kp[c] = X(t.matmul_mx(T.psp[:, 512 * c:512 * c + 128], T.xq[:, e], T.xs[:, e], T.uq[:, 0:128], T.us[:, 0:128], True, True))
+
+    def scores_along(h):
         e = slice(256 * h, 256 * h + 256)
-        wait("v", dx[h])
-        kq = V(v.quantize_mx(T.xq[:, e], T.xs[:, e], T.xb[:, 1024 * h:1024 * h + 1024]))
-        wait("t", k_u, kq)
-        kf[h] = X(t.matmul_mx(T.psf[:, 512 * h:512 * h + 256], T.uq[:, 0:128], T.us[:, 0:128], T.xq[:, e], T.xs[:, e], True, True))
-        for c in (2 * h, 2 * h + 1):
-            e2 = slice(128 * c, 128 * c + 128)
-            kp[c] = X(t.matmul_mx(T.psp[:, 512 * c:512 * c + 128], T.xq[:, e2], T.xs[:, e2], T.uq[:, 0:128], T.us[:, 0:128], True, True))
-        wait("s", kf[h])
+        wait("t", kq[2 * h + 1])
+        k = X(t.matmul_mx(T.psf[:, 512 * h:512 * h + 256], T.uq[:, 0:128], T.us[:, 0:128], T.xq[:, e], T.xs[:, e], True, True))
+        wait("s", k)
         kf[h] = S(s.activation(T.sf[:, e], T.psf[:, 512 * h:512 * h + 256], COPY))
+    for h in range(2):
+        scores_down(2 * h)
+        scores_along(h)
+        scores_down(2 * h + 1)
     km = [None] * 4
     for c in range(4):
         wait("g", kf[c // 2])
-        e2 = slice(128 * c, 128 * c + 128)
-        km[c] = done(g.affine_select(T.sm[:, e2], T.sf[:, e2], [[-1, 128]], OP.is_gt, BIG, 0, 1), "gc")
+        e = slice(128 * c, 128 * c + 128)
+        km[c] = done(g.affine_select(T.sm[:, e], T.sf[:, e], [[-1, 128]], OP.is_gt, BIG, 0, 1), "gc")
 
     cm = [T.cma, T.cmb, T.cmc, T.cmd]
     jk = [0]
@@ -177,42 +194,51 @@ def rank_program(g, core, T, topo):
     V(v.tensor_copy(sp[0], T.psp[:, 0:1]))
     a = V(v.tensor_copy(sp[1], T.psp[:, 512:513]))
     wait("v", a, kf[0])
-    cmp(cm[0][:, 0:256], sf[:, 0:256], sp[0], OP.is_gt)
+    e0 = cmp(cm[0][:, 0:256], sf[:, 0:256], sp[0], OP.is_gt)
+    e0 = total(cm[0], 0, 256, cm[0][:, 384:385], e0)
     cmp(cm[1][:, 0:128], sf[:, 0:128], sp[1], OP.is_ge)
-    cmp(cm[1][:, 128:256], sf[:, 128:256], sp[1], OP.is_gt)
+    e1 = cmp(cm[1][:, 128:256], sf[:, 128:256], sp[1], OP.is_gt)
+    e1 = total(cm[1], 0, 256, cm[1][:, 384:385], e1)
     wait("v", km[0])
-    e0 = cmp(cm[0][:, 256:384], sm[:, 0:128], sp[0], OP.is_equal)
+    cmp(cm[0][:, 256:384], sm[:, 0:128], sp[0], OP.is_equal)
     wait("v", km[1])
-    e1 = cmp(cm[1][:, 256:384], sm[:, 128:256], sp[1], OP.is_equal)
-    e0 = total(cm[0], 0, 384, cm[0][:, 384:385], e0)
-    e1 = total(cm[1], 0, 384, cm[1][:, 384:385], e1)
+    cmp(cm[1][:, 256:384], sm[:, 128:256], sp[1], OP.is_equal)
     wait("v", kp[3])
     V(v.tensor_copy(sp[2], T.psp[:, 1024:1025]))
     a = V(v.tensor_copy(sp[3], T.psp[:, 1536:1537]))
-    wait("v", a, kf[1])
+    wait("v", kf[1])
+    pl = [None] * 3
+    for c, e in ((0, e0), (1, e1)):
+        k = cmp(cm[c][:, 385:641], sf[:, 256:512], sp[c], OP.is_gt)
+        pl[c] = total(cm[c], 256, 641, T.pl1[:, c:c + 1], k, e)
+    wait("v", a)
     cmp(cm[2][:, 0:256], sf[:, 0:256], sp[2], OP.is_ge)
     e2 = cmp(cm[2][:, 256:512], sf[:, 256:512], sp[2], OP.is_gt)
     e2 = total(cm[2], 0, 512, cm[2][:, 640:641], e2)
-    cmp(cm[3][:, 0:384], sf[:, 0:384], sp[3], OP.is_ge)
-    e3 = cmp(cm[3][:, 384:512], sf[:, 384:512], sp[3], OP.is_gt)
-    e3 = total(cm[3], 0, 512, cm[3][:, 640:641], e3)
-    pl = [None] * 4
-    for c, e in ((0, e0), (1, e1)):
-        a = cmp(cm[c][:, 385:641], sf[:, 256:512], sp[c], OP.is_gt)
-        pl[c] = total(cm[c], 384, 641, T.pl1[:, c:c + 1], a, e)
-    for c, e in ((2, e2), (3, e3)):
-        wait("v", km[c])
-        a = cmp(cm[c][:, 512:640], sm[:, 128 * c:128 * c + 128], sp[c], OP.is_equal)
-        pl[c] = total(cm[c], 512, 641, T.pl1[:, c:c + 1], a, e)
+    wait("v", km[2])
+    k2 = cmp(cm[2][:, 512:640], sm[:, 256:384], sp[2], OP.is_equal)
+    k3 = cmp(cm[3][:, 0:384], sf[:, 0:384], sp[3], OP.is_ge)
+    pl[2] = total(cm[2], 512, 641, T.pl1[:, 2:3], k2, e2)
+    k3 = total(cm[3], 0, 384, T.pl1[:, 3:4], k3)
+    cmp(cm[3][:, 384:512], sf[:, 384:512], sp[3], OP.is_gt)
+    wait("v", km[3])
+    a = cmp(cm[3][:, 512:640], sm[:, 384:512], sp[3], OP.is_equal)
+    wait("v", a)
+    e3 = V(v.tensor_reduce(T.pl3[:, 0:1], cm[3][:, 384:641], AxisListType.X, OP.add, negate=bool(odd)))
+    wait("v", *pl)
+    if odd:
+        V(v.tensor_scalar(T.pu1[:, 0:3], T.pl1[:, 0:3], -1.0, 511.0, OP.mult, OP.add))
+    else:
+        V(v.tensor_copy(T.pu1[:, 0:3], T.pl1[:, 0:3]))
+    wait("v", k3, e3)
+    k_pu = V(v.tensor_scalar(T.pu1[:, 3:4], T.pl1[:, 3:4], -1.0 if odd else 1.0, T.pl3[:, 0:1], OP.mult, OP.add))
 
-    def invert(n, ready, cols, vals, lo, low8):
+    def invert(n, ready, cols, vals, lo, scale):
         W = lambda b: T[b + n]
-        wait("v", *ready)
+        wait("v", k_ch, *ready)
         a = V(v.tensor_copy(W("win")[:, 0:512].indirect(W("pu")[:, 0:cols]), vals[:, 0:16 * cols]))
         wait("v", a)
-        a = V(v.tensor_tensor(W("wm")[:, 0:128], W("win")[:, lo:lo + 128], T.mk[:, 0:128], OP.mult))
-        wait("v", a)
-        a = V(v.tensor_tensor_scan(W("sc")[:, 0:128], T.seg[:, 0:128], W("wm")[:, 0:128], 0.0, OP.mult, OP.add))
+        a = V(v.tensor_tensor_scan(W("sc")[:, 0:128], T.ch[:, 0:128], W("win")[:, lo:lo + 128], 0.0, OP.add, OP.max))
         wait("v", a)
         a = V(v.tensor_tensor(W("qa")[0:64, 0:8], W("sc")[0:64, 15:128:16], W("sc")[64:128, 15:128:16], OP.add))
         wait("v", a)
@@ -225,15 +251,8 @@ def rank_program(g, core, T, topo):
         wait("v", a)
         a = V(v.transpose(W("tb")[0:32, 0:32], W("tw")[0:32, 0:32]))
         wait("v", a)
-        src = W("tb")
-        if low8:
-            a = V(v.tensor_copy(T.pin[0:32, 0:8], W("tb")[0:32, 0:8]))
-            wait("v", a)
-            a = V(v.tensor_scalar(T.pia[0:32, 0:8], T.pin[0:32, 0:8], 255, None, OP.bitwise_and))
-            wait("v", a)
-            src = T.pia
         for h in range(4):
-            a = V(v.tensor_copy(W("lst")[32 * h:32 * h + 32, 0:8], src[0:32, 0:8]))
+            a = V(v.tensor_scalar(W("lst")[32 * h:32 * h + 32, 0:8], W("tb")[0:32, 0:8], T.pcq[0:32, 0:1], scale, OP.add, OP.mult))
         return a
 
     def pick(dc, ds, sc, ss, off, ready_c, ready_s):
@@ -256,13 +275,7 @@ def rank_program(g, core, T, topo):
             count["sent"] = count.get("sent", 0) + n
         return (sem_c, n), (sem_s, n)
 
-    odd = rank % 2
-    wait("v", *pl)
-    if odd:
-        a = V(v.tensor_scalar(T.pu1[:, 0:4], T.pl1[:, 0:4], -1.0, 511.0, OP.mult, OP.add))
-    else:
-        a = V(v.tensor_copy(T.pu1[:, 0:4], T.pl1[:, 0:4]))
-    k_l1 = invert("1", (a,), 4, T.vals1, 384 if odd else 0, False)
+    k_l1 = invert("1", (k_pu,), 4, T.vals1, 384 if odd else 0, 2.0)
     a1, b1 = pick(T.c1, T.s1, T.xq[:, 0:512], T.xs[:, 0:512], T.lst1, (k_l1,), (k_l1,))
     mate = T.cores[rank ^ 1]
     in1c, in1s = send(T.c1, T.s1, a1, b1, mate, "h1c", "h1s")
@@ -284,33 +297,39 @@ def rank_program(g, core, T, topo):
     wait("v", a2)
     k_msg = V(v.tensor_copy(T.msg[:, m0:m0 + 4], T.at[:, 0:128:32]))
     wait("g", k_msg)
-    ids, m = [], 0xFFFF
-    for other in (rank ^ 1, rank ^ 2, rank ^ 3):
+    ids, m = [], topo.mask(core, T.cores[rank ^ 2])
+    for other in (rank ^ 2, rank ^ 3):
         dst = T.cores[other]
         rid, pid = topo.addr(dst, core)
         ids.append(DstId(rid=rid, pnc=pid))
         m &= topo.mask(core, dst)
     n = bin(m).count("1")
     view = T.msg[:, m0:m0 + 6]
-    g.remote_dma_fused([RemoteDMATransfer(dst_ids=ids, dma_engine_mask=m, remote_sem=T.sem["hm"], srcs=[view], dsts=[view] * 3)],
+    g.remote_dma_fused([RemoteDMATransfer(dst_ids=ids, dma_engine_mask=m, remote_sem=T.sem["hm"], srcs=[view], dsts=[view] * 2)],
                        local_sem=T.sem["sent"])
-    count["sent"] += n
-    in_msg = ("hm", 3 * n)
+    in_msg = ("hm", 2 * n)
+    rid, pid = topo.addr(mate, core)
+    view = T.msg[:, m0 + 5:m0 + 6]
+    g.remote_dma(view, view, T.sem["hp"], T.sem["sent"], pid, rid, topo.mask(core, mate))
+    in_num = ("hp", len(topo.engines(core, mate)))
+    count["sent"] += n + in_num[1]
 
-    a = V(v.tensor_scalar(T.nb[:, 0:128], T.mk[:, 0:128], -BIG, BIG, OP.mult, OP.add))
+    a = V(v.tensor_scalar(T.mk[:, 0:128], T.ita[:, 0:128], 0.0, None, OP.is_equal))
+    b = V(v.memset(T.hs[:, 0:128], 0.0))
+    wait("v", a)
+    a = V(v.tensor_scalar(T.nb[:, 0:128], T.mk[:, 0:128], BIG, -BIG, OP.mult, OP.add))
     b2 = V(v.tensor_tensor(T.am0[:, 0:128], T.psf[:, 0:128], T.mk[:, 0:128], OP.mult))
     wait("v", a, b2)
     k_am = V(v.tensor_tensor(T.am[:, 0:128], T.am0[:, 0:128], T.nb[:, 0:128], OP.add))
-    k_bas = V(v.tensor_scalar(T.bas[:, 0:8], T.i6[:, 0:8], T.pcf[:, 1:2], 1.0 / 128, OP.add, OP.mult))
+    k_hs = V(v.tensor_scalar(T.hs[:, 0:128:16], T.i6[:, 0:8], T.pcq[:, 1:2], 1.0 / 128, OP.add, OP.mult))
     wait("v", k_i5, k_i7)
     k_eo = V(v.tensor_copy(T.eoff[:, 0:16], T.i5[:, 0:16]))
     V(v.tensor_scalar(T.hm[:, 0:32], T.i7[:, 0:32], T.pcf[:, 2:3], None, OP.is_equal))
     V(v.memset(T.win2[:, 0:512], 0.0))
     V(v.memset(T.ti2[:, 0:32], 0.0))
-    pair = rank // 2
     ca, cb, cx = (T.ca0, T.ca1), (T.cb0, T.cb1), (T.cx0, T.cx1)
     for j in range(2):
-        V(v.tensor_scalar(T.pos[:, j:j + 1], T.pcf[:, 3:4], float(256 * 1024 * (pair ^ j) + 128 * j), None, OP.add))
+        V(v.tensor_scalar(T.pos[:, j:j + 1], T.pcf[:, 3:4], 128.0 * j + 1024.0 * (pair ^ j) / GID, None, OP.add))
         V(v.tensor_copy(ca[j][:, 128:129], T.pcf[:, 3:4]))
         V(v.tensor_scalar(cb[j][:, 128:129], T.pcf[:, 3:4], -1.0, 127.0, OP.mult, OP.add))
     wait("v", dw)
@@ -320,13 +339,11 @@ def rank_program(g, core, T, topo):
     kb = X(t.matmul_mx(T.psf[:, 512:640], T.uq[:, 0:128], T.us[:, 0:128], T.c1[:, 128:256], T.s1[:, 128:256], True, True))
     kbp = X(t.matmul_mx(T.psp[:, 512:640], T.c1[:, 128:256], T.s1[:, 128:256], T.uq[:, 0:128], T.us[:, 0:128], True, True))
     wait("v", kb, k_am)
-    a = V(v.tensor_tensor(T.bc[:, 0:128], T.psf[:, 512:640], T.am[:, 0:128], OP.is_ge if odd else OP.is_gt))
+    a = V(v.tensor_tensor(T.bc[:, 0:128], T.am[:, 0:128], T.psf[:, 512:640], OP.is_gt if odd else OP.is_ge))
+    wait("v", a, k_hs)
+    a = V(v.tensor_tensor_scan(T.bs[:, 0:128], T.hs[:, 0:128], T.bc[:, 0:128], 0.0, OP.max, OP.subtract))
     wait("v", a)
-    a = V(v.tensor_tensor_scan(T.bs[:, 0:128], T.seg[:, 0:128], T.bc[:, 0:128], 0.0, OP.mult, OP.add))
-    wait("v", a, k_bas)
-    a = V(v.tensor_tensor(T.o2f[:, 0:8], T.bs[:, 15:128:16], T.bas[:, 0:8], OP.add))
-    wait("v", a)
-    k_o2 = V(v.tensor_scalar(T.off2[:, 0:8], T.o2f[:, 0:8], 128.0, None, OP.mult))
+    k_o2 = V(v.tensor_scalar(T.off2[:, 0:8], T.bs[:, 15:128:16], 128.0, None, OP.mult))
     a2, b2 = pick(T.c2, T.s2, T.c1[:, 0:256], T.s1[:, 0:256], T.off2, (k_o2, in1c), (k_o2, in1s))
     in2c, in2s = send(T.c2, T.s2, a2, b2, T.cores[rank ^ 2], "h2c", "h2s")
 
@@ -350,64 +367,66 @@ def rank_program(g, core, T, topo):
     wait("v", in_msg)
     V(v.tensor_tensor(ps[1], col(2 * j1, 4), col(2 * j1 + 1, 4), OP.max))
     a = V(v.tensor_tensor(sel[1], col(2 * j1 + 1, 4), col(2 * j1, 4), OP.is_gt))
-    for j in range(2):
-        b = V(v.tensor_scalar(T.cp0[:, j:j + 1], col(2 * (pair ^ j) + 1, 5), col(2 * (pair ^ j), 5), 512.0, OP.subtract, OP.add))
-    wait("v", a, b)
+    wait("v", a)
     for f in range(2):
         k = cmp(cx[1][:, 128 * f:128 * f + 128], fr[f], ps[1], OP.is_ge if pair == 0 else OP.is_gt)
     ka[5] = total(cx[1], 0, 256, acc[5], k)
-    for j in range(2):
-        b = V(v.tensor_scalar(T.cp1[:, j:j + 1], T.cp0[:, j:j + 1], sel[j], col(2 * (pair ^ j), 5), OP.mult, OP.add))
-    wait("v", b)
-    for j in range(2):
-        kcp = V(v.tensor_scalar(T.cp[:, j:j + 1], T.cp1[:, j:j + 1], 256.0, T.pos[:, j:j + 1], OP.mult, OP.add))
     wait("v", ky)
     k = V(v.transpose(T.fs[:, 0:256], T.yx[:, 0:256]))
+    wait("v", in_num)
+    for j in range(2):
+        b = V(v.tensor_scalar(T.cp0[:, j:j + 1], col(2 * (pair ^ j) + 1, 5), col(2 * (pair ^ j), 5), 512.0, OP.subtract, OP.add))
     wait("v", k)
     k = cmp(cx[0][:, 0:256], T.fs[:, 0:256], ps[0], OP.is_ge if pair == 1 else OP.is_gt)
-    a = cmp(ca[1][:, 0:128], T.fs[:, 128:256], ps[1], OP.is_gt)
-    b = cmp(cb[1][:, 0:128], T.fs[:, 0:128], ps[1], OP.is_ge)
+    ka[4] = total(cx[0], 0, 256, acc[4], k)
+    wait("v", b)
+    for j in range(2):
+        b = V(v.tensor_scalar(T.cp1[:, j:j + 1], T.cp0[:, j:j + 1], sel[j], col(2 * (pair ^ j), 5), OP.mult, OP.add))
+    k = cmp(ca[1][:, 0:128], T.fs[:, 128:256], ps[1], OP.is_gt)
+    ka[2] = total(ca[1], 0, 129, acc[2], k)
+    wait("v", b)
+    for j in range(2):
+        kcp = V(v.tensor_scalar(T.cp[:, j:j + 1], T.cp1[:, j:j + 1], 1.0 / GID, T.pos[:, j:j + 1], OP.mult, OP.add))
+    k = cmp(cb[1][:, 0:128], T.fs[:, 0:128], ps[1], OP.is_ge)
     wait("s", kcp)
     for j in range(2):
         kz = S(s.activation(T.zx[:, 32 * j:32 * j + 32], T.hm[:, 0:32], COPY, scale=T.cp[:, j:j + 1]))
-    ka[4] = total(cx[0], 0, 256, acc[4], k)
-    ka[2] = total(ca[1], 0, 129, acc[2], a)
-    ka[3] = total(cb[1], 0, 129, acc[3], b)
-    wait("v", kz)
-    a = V(v.transpose(T.zt[:, 0:64], T.zx[:, 0:64]))
+    ka[3] = total(cb[1], 0, 129, acc[3], k)
     wait("v", ka[0], ka[1])
     V(v.tensor_scalar(T.dd[:, 0:1], acc[1], acc[0], sel[0], OP.subtract, OP.mult))
+    wait("v", kz)
+    a = V(v.transpose(T.zt[:, 0:64], T.zx[:, 0:64]))
+    wait("v", ka[2], ka[3])
+    b = V(v.tensor_scalar(T.dd[:, 1:2], acc[3], acc[2], sel[1], OP.subtract, OP.mult))
     wait("v", a)
     for j in range(2):
-        kv = V(v.tensor_tensor(T.vals2[:, 16 * j:16 * j + 16], T.zt[:, 32 * j:32 * j + 16], T.zt[:, 32 * j + 16:32 * j + 32], OP.add))
-    wait("v", ka[2], ka[3])
-    a = V(v.tensor_scalar(T.dd[:, 1:2], acc[3], acc[2], sel[1], OP.subtract, OP.mult))
-    wait("v", a, ka[4], ka[5])
+        V(v.tensor_tensor(T.vals2[:, 16 * j:16 * j + 16], T.zt[:, 32 * j:32 * j + 16], T.zt[:, 32 * j + 16:32 * j + 32], OP.add))
+    wait("v", b, ka[4], ka[5])
     for j in range(2):
         kv = V(v.tensor_scalar(T.pu2[:, j:j + 1], T.dd[:, j:j + 1], acc[2 * j], acc[4 + j], OP.add, OP.add))
-    k_l2 = invert("2", (kv,), 2, T.vals2, 0, True)
+    k_l2 = invert("2", (kv,), 2, T.vals2, 0, 1.0)
 
     a3, b3 = pick(T.c3, T.s3, T.c2[:, 0:256], T.s2[:, 0:256], T.lst2, (k_l2, in2c), (k_l2, in2s))
     wait("t", a3, b3, k_w)
     ko = [X(t.matmul_mx(T.psp[:, 512 * (o + 2):512 * (o + 2) + 128], T.wq[:, 128 * o:128 * o + 128], T.ws[:, 128 * o:128 * o + 128],
                         T.c3[:, 0:128], T.s3[:, 0:128], True, True)) for o in range(2)]
-    a = V(v.tensor_copy(T.idn[0:32, 0:16], T.tw2[0:32, 0:16]))
+    a = V(v.tensor_scalar(T.idn[0:32, 0:16], T.tw2[0:32, 0:16], float(GID), None, OP.mult))
     wait("v", a)
-    V(v.tensor_scalar(T.idr[0:32, 0:16], T.idn[0:32, 0:16], 17, None, OP.arith_shift_right))
-    a = V(v.tensor_scalar(T.idc[0:32, 0:16], T.idn[0:32, 0:16], 8, 511, OP.arith_shift_right, OP.bitwise_and))
+    V(v.tensor_scalar(T.idr[0:32, 0:16], T.idn[0:32, 0:16], 9, 3, OP.arith_shift_right, OP.bitwise_and))
+    a = V(v.tensor_scalar(T.idc[0:32, 0:16], T.idn[0:32, 0:16], 511, None, OP.bitwise_and))
     wait("v", a)
     V(v.tensor_copy(T.idf[0:32, 0:16], T.idr[0:32, 0:16]))
     kid = V(v.tensor_copy(T.idf[0:32, 16:32], T.idc[0:32, 0:16]))
-    wait("v", ko[0])
-    ky0 = V(v.tensor_copy(T.yb[:, 0:128], T.psp[:, 1024:1152]))
-    wait("s", ko[1])
-    ky1 = S(s.activation(T.yb[:, 128:256], T.psp[:, 1536:1664], COPY))
-    wait("y", ky0)
-    d0 = done(y.dma_start(T.y[:, 0:128], T.yb[:, 0:128]), "dy0", 16)
-    wait("s", ky1)
-    d1 = done(s.dma_start(T.y[:, 128:256], T.yb[:, 128:256]), "dy1", 16)
+    wait("s", ko[0])
+    ky0 = S(s.activation(T.yb[:, 0:128], T.psp[:, 1024:1152], COPY))
+    wait("v", ko[1])
+    ky1 = V(v.tensor_copy(T.yb[:, 128:256], T.psp[:, 1536:1664]))
+    wait("s", ky0)
+    d0 = done(s.dma_start(T.y[:, 0:128], T.yb[:, 0:128]), "dy0", 16)
     wait("y", kid)
     for row in range(2):
         d2 = done(y.dma_start(T["id"][row:row + 1, 0:128], T.idf[0:8, 16 * row:16 * row + 16]), "did", 16)
-    wait("g", ("sent", count["sent"]), in1c, in1s, in2c, in2s, in_msg, du, dx[0], dx[1], dw,
+    wait("y", ky1)
+    d1 = done(y.dma_start(T.y[:, 128:256], T.yb[:, 128:256]), "dy1", 16)
+    wait("g", ("sent", count["sent"]), in1c, in1s, in2c, in2s, in_msg, in_num, du, *dx, dw,
          ("gc", count["gc"]), ("v", count["v"]), ("s", count["s"]), ("t", count["t"]), d0, d1, d2)

@@ -3,62 +3,55 @@ from concourse.mybir import dt, AluOpType, AxisListType, ActivationFunctionType
 
 OP = AluOpType
 COPY = ActivationFunctionType.Copy
+IDENT = ActivationFunctionType.Identity
+SQUARE = ActivationFunctionType.Square
 K = 128
 BIG = 1e29
 LIFT = 256.0
 GID = 4096
 
 SCRATCH = {
-    "ub": ("sbuf", [128, 16], "bfloat16"),
-    "ur": ("sbuf", [128, 512], "bfloat16"),
-    "uq": ("sbuf", [128, 128], "float8_e4m3fn_x4"),
-    "us": ("sbuf", [128, 128], "uint8"),
+    "ur": ("sbuf", [128, 512], "bfloat16"), "zoff": ("sbuf", [128, 8], "uint16"),
+    "uq0": ("sbuf", [128, 128], "float8_e4m3fn_x4"), "us0": ("sbuf", [128, 128], "uint8"),
+    "uq": ("sbuf", [128, 128], "float8_e4m3fn_x4"), "us": ("sbuf", [128, 128], "uint8"),
     "xb": ("sbuf", [128, 2048], "bfloat16"),
-    "xq": ("sbuf", [128, 512], "float8_e4m3fn_x4"),
-    "xs": ("sbuf", [128, 512], "uint8"),
+    "xq": ("sbuf", [128, 512], "float8_e4m3fn_x4"), "xs": ("sbuf", [128, 512], "uint8"),
     "wb": ("sbuf", [128, 1024], "bfloat16"),
-    "wq": ("sbuf", [128, 256], "float8_e4m3fn_x4"),
-    "ws": ("sbuf", [128, 256], "uint8"),
-    "c1": ("sbuf", [128, 256], "float8_e4m3fn_x4"),
-    "s1": ("sbuf", [128, 256], "uint8"),
-    "c2": ("sbuf", [128, 256], "float8_e4m3fn_x4"),
-    "s2": ("sbuf", [128, 256], "uint8"),
-    "c3": ("sbuf", [128, 128], "float8_e4m3fn_x4"),
-    "s3": ("sbuf", [128, 128], "uint8"),
-    "yb": ("sbuf", [128, 256], "float32"),
+    "wq": ("sbuf", [128, 256], "float8_e4m3fn_x4"), "ws": ("sbuf", [128, 256], "uint8"),
+    "c1": ("sbuf", [128, 256], "float8_e4m3fn_x4"), "s1": ("sbuf", [128, 256], "uint8"),
+    "c2": ("sbuf", [128, 256], "float8_e4m3fn_x4"), "s2": ("sbuf", [128, 256], "uint8"),
+    "yw0": ("sbuf", [128, 256], "float32"), "yw1": ("sbuf", [128, 256], "float32"),
+    "yb0": ("sbuf", [128, 128], "float32"), "yb1": ("sbuf", [128, 128], "float32"),
     "psf": ("psum", [128, 2048], "float32"),
     "psp": ("psum", [128, 2048], "float32"),
-    "ip": ("sbuf", [128, 32], "int32"), "ipa": ("sbuf", [128, 32], "int32"), "uoff": ("sbuf", [128, 32], "uint16"),
+    "ip": ("sbuf", [128, 4], "int32"), "pt": ("sbuf", [128, 4], "float32"),
     "it": ("sbuf", [128, 128], "int32"), "ita": ("sbuf", [128, 128], "int32"),
-    "mk": ("sbuf", [128, 128], "float32"), "nb": ("sbuf", [128, 128], "float32"),
+    "nb0": ("sbuf", [128, 128], "float32"), "nb": ("sbuf", [128, 128], "float32"),
     "ch0": ("sbuf", [128, 128], "float32"), "ch1": ("sbuf", [128, 128], "float32"), "ch": ("sbuf", [128, 128], "float32"),
     "i3": ("sbuf", [128, 64], "float32"), "vals1": ("sbuf", [128, 64], "float32"),
     "i5": ("sbuf", [128, 16], "int32"), "eoff": ("sbuf", [128, 16], "uint16"),
     "i6": ("sbuf", [128, 8], "float32"), "gm": ("sbuf", [128, 8], "float32"), "hs": ("sbuf", [128, 128], "float32"),
     "i7": ("sbuf", [128, 32], "float32"), "hm": ("sbuf", [128, 32], "float32"),
-    "pca": ("sbuf", [128, 4], "int32"), "pcf": ("sbuf", [128, 4], "float32"), "pcq": ("sbuf", [128, 2], "float32"),
-    "pos": ("sbuf", [128, 2], "float32"),
-    "sf": ("sbuf", [128, 512], "float32"), "sp": ("sbuf", [128, 4], "float32"), "sm": ("sbuf", [128, 512], "float32"),
-    "cma": ("sbuf", [128, 644], "float32"), "cmb": ("sbuf", [128, 644], "float32"),
-    "cmc": ("sbuf", [128, 644], "float32"), "cmd": ("sbuf", [128, 644], "float32"),
+    "pca": ("sbuf", [128, 3], "int32"), "pcf": ("sbuf", [128, 3], "float32"), "pcq": ("sbuf", [128, 2], "float32"),
+    "pct": ("sbuf", [128, 2], "float32"),
+    "sf": ("sbuf", [128, 512], "float32"), "sm": ("sbuf", [128, 512], "float32"),
+    "cma": ("sbuf", [128, 648], "float32"), "cmb": ("sbuf", [128, 648], "float32"),
+    "cmc": ("sbuf", [128, 648], "float32"), "cmd": ("sbuf", [128, 648], "float32"),
     "junk": ("sbuf", [128, 4096], "bfloat16"),
-    "pl1": ("sbuf", [128, 4], "float32"), "pl3": ("sbuf", [128, 1], "float32"),
+    "pl1": ("sbuf", [128, 4], "float32"),
     "msg": ("sbuf", [128, 32], "float32"),
     "at": ("sbuf", [128, 128], "float32"), "o1f": ("sbuf", [128, 8], "float32"), "o1g": ("sbuf", [128, 8], "float32"),
-    "am0": ("sbuf", [128, 128], "float32"), "am": ("sbuf", [128, 128], "float32"),
+    "am": ("sbuf", [128, 128], "float32"),
     "bc": ("sbuf", [128, 128], "float32"), "bs": ("sbuf", [128, 128], "float32"),
     "off2": ("sbuf", [128, 8], "uint16"),
     "yx": ("sbuf", [128, 256], "float32"), "fs": ("sbuf", [128, 256], "float32"),
-    "ps": ("sbuf", [128, 2], "float32"), "sel": ("sbuf", [128, 2], "float32"),
-    "ca0": ("sbuf", [128, 130], "bfloat16"), "ca1": ("sbuf", [128, 130], "bfloat16"),
-    "cb0": ("sbuf", [128, 130], "bfloat16"), "cb1": ("sbuf", [128, 130], "bfloat16"),
-    "cx0": ("sbuf", [128, 256], "bfloat16"), "cx1": ("sbuf", [128, 256], "bfloat16"),
-    "acc": ("sbuf", [128, 6], "float32"), "dd": ("sbuf", [128, 2], "float32"),
-    "cp0": ("sbuf", [128, 2], "float32"), "cp1": ("sbuf", [128, 2], "float32"), "cp": ("sbuf", [128, 2], "float32"),
+    "ps": ("sbuf", [128, 2], "float32"), "sel": ("sbuf", [128, 2], "float32"), "nsel": ("sbuf", [128, 2], "float32"),
+    "vd": ("sbuf", [128, 2], "float32"), "cp": ("sbuf", [128, 2], "float32"),
+    "ba": ("sbuf", [128, 520], "float32"), "bb": ("sbuf", [128, 520], "float32"),
+    "pl2": ("sbuf", [128, 2], "float32"),
     "zx": ("sbuf", [128, 64], "float32"), "zt": ("sbuf", [128, 64], "float32"),
     "vals2": ("sbuf", [128, 32], "float32"),
-    "idn": ("sbuf", [32, 16], "int32"), "idr": ("sbuf", [32, 16], "int32"), "idc": ("sbuf", [32, 16], "int32"),
-    "idf": ("sbuf", [32, 32], "float32"),
+    "idn": ("sbuf", [32, 16], "int32"), "idi": ("sbuf", [32, 32], "int32"), "idf": ("sbuf", [32, 32], "float32"),
 }
 for _n in ("1", "2"):
     SCRATCH["pu" + _n] = ("sbuf", [128, 4], "uint16")
@@ -70,7 +63,7 @@ for _n in ("1", "2"):
     SCRATCH["lst" + _n] = ("sbuf", [128, 8], "uint16")
 
 SEMAPHORES = ["v", "s", "t", "gc", "du", "dx0", "dx1", "dx2", "dx3", "dw", "dy0", "dy1", "did",
-              "h1c", "h1s", "h2c", "h2s", "hm", "hp", "sent"]
+              "h1c", "h1s", "h2c", "h2s", "hm", "sent"]
 
 
 def rank_program(g, core, T, topo):
@@ -80,7 +73,8 @@ def rank_program(g, core, T, topo):
     v, s, t, y = g.vector, g.scalar, g.tensor, g.sync
     queue = {"g": g, "v": v, "s": s, "t": t, "y": y}
     count, waited = {}, {}
-    odd, pair = rank % 2, rank // 2
+    odd, P, Q = rank % 2, rank // 2, (rank // 2) ^ 1
+    own, arr = slice(K * P, K * P + K), slice(K * Q, K * Q + K)
 
     def done(ins, sem, n=1):
         ins.then_inc(T.sem[sem], n)
@@ -100,7 +94,7 @@ def rank_program(g, core, T, topo):
     def S(ins): return done(ins, "s")
     def X(ins): return done(ins, "t")
 
-    du = done(s.dma_start(T.ub[:, 0:4], T.u[:, 0:4]), "du", 16)
+    du = done(s.dma_start(T.ur[:, 0:8], T.u[:, 0:8]), "du", 16)
     dx = [done(y.dma_start(T.xb[:, 512 * d:512 * d + 512], T.x[:, 512 * d:512 * d + 512]), "dx%d" % d, 16) for d in range(4)]
     dw = done(y.dma_start(T.wb[:, 0:1024], T.w[:, 0:1024]), "dw", 16)
 
@@ -108,72 +102,73 @@ def rank_program(g, core, T, topo):
         if flt:
             return done(g.iota(buf, pattern, base, cm, allow_small_or_imprecise_dtypes=True), "gc")
         return done(g.iota(buf, pattern, base, cm), "gc")
-    k_ip = iota(T.ip[:, 0:32], [[0, 32]], 0, 1)
-    k_i3 = iota(T.i3[:, 0:64], [[128, 4], [1, 16]], 0, 0, True)
     k_it = iota(T.it[:, 0:128], [[1, 128]], 128, -1)
+    k_ip = iota(T.ip[:, 0:4], [[0, 4]], 0, 1)
+    k_i3 = iota(T.i3[:, 0:64], [[128, 4], [1, 16]], 0, 0, True)
     k_i6 = iota(T.i6[:, 0:8], [[16, 8]], 0, 0, True)
+    k_pt = iota(T.pt[:, 0:4], [[0, 4]], 0, 1, True)
     k_i5 = iota(T.i5[:, 0:16], [[8, 2], [1, 4], [0, 2]], 0, 0)
     k_i7 = iota(T.i7[:, 0:32], [[16, 2], [0, 16]], 0, 0, True)
 
+    k_ur = V(v.memset(T.ur[:, 8:512], 0.0))
+    k_zo = V(v.memset(T.zoff[:, 0:8], 0))
     V(v.memset(T.win1[:, 0:512], 0.0))
-    V(v.memset(T.ti1[:, 0:32], 0.0))
-    V(v.memset(T.cmd[:, 640:641], -511.0 if odd else 0.0))
-    wait("v", k_ip)
-    a = V(v.tensor_scalar(T.ipa[:, 0:32], T.ip[:, 0:32], 3, None, OP.bitwise_and))
-    V(v.tensor_scalar(T.pca[:, 0:1], T.ip[:, 0:1], 112, None, OP.bitwise_and))
-    V(v.tensor_scalar(T.pca[:, 1:2], T.ip[:, 0:1], 15, None, OP.bitwise_and))
-    V(v.tensor_scalar(T.pca[:, 2:3], T.ip[:, 0:1], 16, None, OP.bitwise_and))
-    b = V(v.tensor_copy(T.pca[:, 3:4], T.ip[:, 0:1]))
-    wait("v", b)
-    k_uo = V(v.tensor_copy(T.uoff[:, 0:32], T.ipa[:, 0:32]))
-    b = V(v.tensor_copy(T.pcf[:, 0:4], T.pca[:, 0:4]))
-    wait("v", b, k_i3)
-    V(v.tensor_scalar(T.vals1[:, 0:64], T.i3[:, 0:64], T.pcf[:, 0:1], 0.5, OP.add, OP.mult))
-    V(v.tensor_scalar(T.pcq[:, 0:1], T.pcf[:, 1:2], 15.0, -8 * LIFT, OP.is_lt, OP.mult))
-    V(v.tensor_scalar(T.pcq[:, 1:2], T.pcf[:, 1:2], 128.0, None, OP.add))
     wait("v", k_it)
-    a = V(v.tensor_scalar(T.ita[:, 0:128], T.it[:, 0:128], 15, None, OP.bitwise_and))
-    wait("v", a)
-    V(v.tensor_scalar(T.ch0[:, 0:128], T.ita[:, 0:128], 0.0, -65536.0, OP.is_equal, OP.mult))
+    k = V(v.tensor_scalar(T.ita[:, 0:128], T.it[:, 0:128], 15, None, OP.bitwise_and))
+    wait("v", k)
+    k_d = V(v.tensor_scalar(T.ch0[:, 0:128], T.ita[:, 0:128], 2.0, None, OP.min))
 
-    wait("s", k_uo, du)
-    ks = S(s.activation(T.ur[:, 256:512], T.ub[:, 0:4].indirect(T.uoff[:, 16:32]), COPY))
-    wait("v", du, k_uo)
-    a = V(v.tensor_copy(T.ur[:, 0:256], T.ub[:, 0:4].indirect(T.uoff[:, 0:16])))
-    wait("v", a, ks)
-    k_u = V(v.quantize_mx(T.uq[:, 0:128], T.us[:, 0:128], T.ur[:, 0:512]))
+    wait("v", du, k_ur)
+    k_u0 = V(v.quantize_mx(T.uq0[:, 0:128], T.us0[:, 0:128], T.ur[:, 0:512]))
+    wait("v", k_u0, k_zo)
+    k_uc = V(v.tensor_copy(T.uq[:, 0:128].bitcast(dt.uint32), T.uq0[:, 0:128].bitcast(dt.uint32).indirect(T.zoff[:, 0:8])))
+    wait("s", k_u0)
+    k_us = S(s.activation(T.us[:, 0:128], T.us0[:, 0:128].indirect(T.zoff[:, 0:8]), COPY))
+    k = S(s.activation(T.ch1[:, 0:128], T.ch0[:, 0:128], SQUARE, bias=-1.25))
+    wait("s", k)
+    k_ch = S(s.activation(T.ch[:, 0:128], T.ch1[:, 0:128], IDENT, bias=1.125 * LIFT, scale=-2 * LIFT))
 
     kq = [None] * 4
-    for d in range(4):
+
+    def quant(d):
         e = slice(128 * d, 128 * d + 128)
         wait("v", dx[d])
         kq[d] = V(v.quantize_mx(T.xq[:, e], T.xs[:, e], T.xb[:, 512 * d:512 * d + 512]))
-        if d == 0:
-            k_ch = V(v.tensor_scalar(T.ch1[:, 0:128], T.ita[:, 0:128], 1.0, LIFT, OP.is_equal, OP.mult))
-        if d == 1:
-            wait("v", k_ch)
-            k_ch = V(v.tensor_tensor(T.ch[:, 0:128], T.ch0[:, 0:128], T.ch1[:, 0:128], OP.add))
-    kp, kf = [None] * 4, [None] * 2
+    quant(0)
+    wait("v", k_ip)
+    V(v.tensor_scalar(T.pca[:, 0:1], T.ip[:, 0:1], 112, None, OP.bitwise_and))
+    V(v.tensor_scalar(T.pca[:, 1:2], T.ip[:, 0:1], 15, None, OP.bitwise_and))
+    b = V(v.tensor_scalar(T.pca[:, 2:3], T.ip[:, 0:1], 16, None, OP.bitwise_and))
+    quant(1)
+    wait("v", b)
+    b = V(v.tensor_copy(T.pcf[:, 0:3], T.pca[:, 0:3]))
+    wait("v", b, k_i3)
+    V(v.tensor_scalar(T.pcq[:, 0:1], T.pcf[:, 1:2], 15.0, -8 * LIFT, OP.is_lt, OP.mult))
+    V(v.tensor_scalar(T.vals1[:, 0:64], T.i3[:, 0:64], T.pcf[:, 0:1], 0.5, OP.add, OP.mult))
+    quant(2)
 
-    def scores_down(c):
+    kp, kh, kf, km = [None] * 4, [None] * 2, [None] * 4, [None] * 4
+
+    def down(c):
         e = slice(128 * c, 128 * c + 128)
-        wait("t", k_u, kq[c])
-        kp[c] = X(t.matmul_mx(T.psp[:, 512 * c:512 * c + 128], T.xq[:, e], T.xs[:, e], T.uq[:, 0:128], T.us[:, 0:128], True, True))
+        wait("t", k_u0, kq[c])
+        kp[c] = X(t.matmul_mx(T.psp[:, 512 * c:512 * c + 128], T.xq[:, e], T.xs[:, e], T.uq0[:, 0:128], T.us0[:, 0:128], True, True))
 
-    def scores_along(h):
+    def half(h):
         e = slice(256 * h, 256 * h + 256)
-        wait("t", kq[2 * h + 1])
-        k = X(t.matmul_mx(T.psf[:, 512 * h:512 * h + 256], T.uq[:, 0:128], T.us[:, 0:128], T.xq[:, e], T.xs[:, e], True, True))
-        wait("s", k)
-        kf[h] = S(s.activation(T.sf[:, e], T.psf[:, 512 * h:512 * h + 256], COPY))
-    for h in range(2):
-        scores_down(2 * h)
-        scores_along(h)
-        scores_down(2 * h + 1)
-    km = [None] * 4
-    for c in range(4):
-        wait("g", kf[c // 2])
+        wait("t", k_uc, k_us, kq[2 * h + 1])
+        kh[h] = X(t.matmul_mx(T.psf[:, 512 * h:512 * h + 256], T.uq[:, 0:128], T.us[:, 0:128], T.xq[:, e], T.xs[:, e], True, True))
+
+    def block(c):
         e = slice(128 * c, 128 * c + 128)
+        o = 512 * (2 + c % 2)
+        wait("t", k_uc, k_us, kq[c])
+        if c > 1:
+            wait("t", kf[c - 2])
+        k = X(t.matmul_mx(T.psf[:, o:o + 128], T.uq[:, 0:128], T.us[:, 0:128], T.xq[:, e], T.xs[:, e], True, True))
+        wait("s", k)
+        kf[c] = S(s.activation(T.sf[:, e], T.psf[:, o:o + 128], COPY))
+        wait("g", kf[c])
         km[c] = done(g.affine_select(T.sm[:, e], T.sf[:, e], [[-1, 128]], OP.is_gt, BIG, 0, 1), "gc")
 
     cm = [T.cma, T.cmb, T.cmc, T.cmd]
@@ -186,57 +181,67 @@ def rank_program(g, core, T, topo):
         jk[0] = jk[0] + n if jk[0] + n + 700 <= 4096 else 0
         return r
 
-    def cmp(out, src, col, op):
-        return V(v.tensor_scalar(out, src, col, None, op))
-    sp = [T.sp[:, c:c + 1] for c in range(4)]
-    sf, sm = T.sf, T.sm
+    def cmp(out, src, col, op, weight=None):
+        if weight is None:
+            return V(v.tensor_scalar(out, src, col, None, op))
+        return V(v.tensor_scalar(out, src, col, weight, op, OP.mult))
+    sp = [T.psp[:, 512 * c:512 * c + 1] for c in range(4)]
+    h0, h1, sm = T.psf[:, 0:256], T.psf[:, 512:768], T.sm
+    down(0)
+    block(0)
+    half(0)
+    down(1)
+    block(1)
+    down(2)
+    wait("v", kp[0], kh[0])
+    cmp(cm[0][:, 0:256], h0, sp[0], OP.is_gt)
+    quant(3)
+    half(1)
     wait("v", kp[1])
-    V(v.tensor_copy(sp[0], T.psp[:, 0:1]))
-    a = V(v.tensor_copy(sp[1], T.psp[:, 512:513]))
-    wait("v", a, kf[0])
-    e0 = cmp(cm[0][:, 0:256], sf[:, 0:256], sp[0], OP.is_gt)
-    e0 = total(cm[0], 0, 256, cm[0][:, 384:385], e0)
-    cmp(cm[1][:, 0:128], sf[:, 0:128], sp[1], OP.is_ge)
-    e1 = cmp(cm[1][:, 128:256], sf[:, 128:256], sp[1], OP.is_gt)
-    e1 = total(cm[1], 0, 256, cm[1][:, 384:385], e1)
+    cmp(cm[1][:, 0:128], T.psf[:, 0:128], sp[1], OP.is_ge)
+    k = cmp(cm[1][:, 128:256], T.psf[:, 128:256], sp[1], OP.is_gt)
+    e1 = total(cm[1], 0, 256, cm[1][:, 256:257], k)
     wait("v", km[0])
-    cmp(cm[0][:, 256:384], sm[:, 0:128], sp[0], OP.is_equal)
+    k = cmp(cm[0][:, 256:384], sm[:, 0:128], sp[0], OP.is_equal)
+    e0 = total(cm[0], 0, 384, cm[0][:, 384:385], k)
+    block(2)
+    down(3)
+    wait("v", kp[2])
+    cmp(cm[2][:, 0:256], h0, sp[2], OP.is_ge)
+    wait("v", kh[1])
+    k = cmp(cm[2][:, 256:512], h1, sp[2], OP.is_gt)
+    e2 = total(cm[2], 0, 512, cm[2][:, 512:513], k)
+    k = cmp(cm[0][:, 385:641], h1, sp[0], OP.is_gt)
+    block(3)
+    total(cm[0], 384, 641, T.pl1[:, 0:1], k, e0)
+    cmp(cm[1][:, 257:513], h1, sp[1], OP.is_gt)
     wait("v", km[1])
-    cmp(cm[1][:, 256:384], sm[:, 128:256], sp[1], OP.is_equal)
+    k = cmp(cm[1][:, 513:641], sm[:, 128:256], sp[1], OP.is_equal)
+    pl = total(cm[1], 256, 641, T.pl1[:, 1:2], k, e1)
     wait("v", kp[3])
-    V(v.tensor_copy(sp[2], T.psp[:, 1024:1025]))
-    a = V(v.tensor_copy(sp[3], T.psp[:, 1536:1537]))
-    wait("v", kf[1])
-    pl = [None] * 3
-    for c, e in ((0, e0), (1, e1)):
-        k = cmp(cm[c][:, 385:641], sf[:, 256:512], sp[c], OP.is_gt)
-        pl[c] = total(cm[c], 256, 641, T.pl1[:, c:c + 1], k, e)
-    wait("v", a)
-    cmp(cm[2][:, 0:256], sf[:, 0:256], sp[2], OP.is_ge)
-    e2 = cmp(cm[2][:, 256:512], sf[:, 256:512], sp[2], OP.is_gt)
-    e2 = total(cm[2], 0, 512, cm[2][:, 640:641], e2)
+    k = cmp(cm[3][:, 0:256], h0, sp[3], OP.is_ge)
+    e3 = total(cm[3], 0, 256, cm[3][:, 640:641], k)
+    cmp(cm[3][:, 256:384], T.psf[:, 512:640], sp[3], OP.is_ge)
+    cmp(cm[3][:, 384:512], T.psf[:, 640:768], sp[3], OP.is_gt)
     wait("v", km[2])
-    k2 = cmp(cm[2][:, 512:640], sm[:, 256:384], sp[2], OP.is_equal)
-    k3 = cmp(cm[3][:, 0:384], sf[:, 0:384], sp[3], OP.is_ge)
-    pl[2] = total(cm[2], 512, 641, T.pl1[:, 2:3], k2, e2)
-    k3 = total(cm[3], 0, 384, T.pl1[:, 3:4], k3)
-    cmp(cm[3][:, 384:512], sf[:, 384:512], sp[3], OP.is_gt)
+    a = cmp(cm[2][:, 513:641], sm[:, 256:384], sp[2], OP.is_equal)
     wait("v", km[3])
-    a = cmp(cm[3][:, 512:640], sm[:, 384:512], sp[3], OP.is_equal)
-    wait("v", a)
-    e3 = V(v.tensor_reduce(T.pl3[:, 0:1], cm[3][:, 384:641], AxisListType.X, OP.add, negate=bool(odd)))
-    wait("v", *pl)
+    b = cmp(cm[3][:, 512:640], sm[:, 384:512], sp[3], OP.is_equal)
+    V(v.memset(T.ti1[:, 0:32], 0.0))
+    wait("v", a, e2)
+    V(v.tensor_reduce(T.pl1[:, 2:3], cm[2][:, 512:641], AxisListType.X, OP.add))
+    wait("v", b, e3)
+    a = V(v.tensor_reduce(T.pl1[:, 3:4], cm[3][:, 256:641], AxisListType.X, OP.add))
+    wait("v", a, pl)
     if odd:
-        V(v.tensor_scalar(T.pu1[:, 0:3], T.pl1[:, 0:3], -1.0, 511.0, OP.mult, OP.add))
+        k_pu = V(v.tensor_scalar(T.pu1[:, 0:4], T.pl1[:, 0:4], -1.0, 511.0, OP.mult, OP.add))
     else:
-        V(v.tensor_copy(T.pu1[:, 0:3], T.pl1[:, 0:3]))
-    wait("v", k3, e3)
-    k_pu = V(v.tensor_scalar(T.pu1[:, 3:4], T.pl1[:, 3:4], -1.0 if odd else 1.0, T.pl3[:, 0:1], OP.mult, OP.add))
+        k_pu = V(v.tensor_copy(T.pu1[:, 0:4], T.pl1[:, 0:4]))
 
-    def invert(n, ready, cols, vals, lo, scale):
+    def invert(n, ready, cols, width, vals, lo, scale, fill):
         W = lambda b: T[b + n]
         wait("v", k_ch, *ready)
-        a = V(v.tensor_copy(W("win")[:, 0:512].indirect(W("pu")[:, 0:cols]), vals[:, 0:16 * cols]))
+        a = V(v.tensor_copy(W("win")[:, 0:width].indirect(W("pu")[:, 0:cols]), vals[:, 0:16 * cols]))
         wait("v", a)
         a = V(v.tensor_tensor_scan(W("sc")[:, 0:128], T.ch[:, 0:128], W("win")[:, lo:lo + 128], 0.0, OP.add, OP.max))
         wait("v", a)
@@ -250,6 +255,7 @@ def rank_program(g, core, T, topo):
         a = V(v.tensor_tensor(W("tw")[0:32, 16:32], W("to")[0:32, 0:16], W("to")[0:32, 16:32], OP.add))
         wait("v", a)
         a = V(v.transpose(W("tb")[0:32, 0:32], W("tw")[0:32, 0:32]))
+        fill()
         wait("v", a)
         for h in range(4):
             a = V(v.tensor_scalar(W("lst")[32 * h:32 * h + 32, 0:8], W("tb")[0:32, 0:8], T.pcq[0:32, 0:1], scale, OP.add, OP.mult))
@@ -257,176 +263,162 @@ def rank_program(g, core, T, topo):
 
     def pick(dc, ds, sc, ss, off, ready_c, ready_s):
         wait("v", *ready_c)
-        a = V(v.tensor_copy(dc[:, 0:K].bitcast(dt.uint32), sc.bitcast(dt.uint32).indirect(off[:, 0:8])))
+        a = V(v.tensor_copy(dc.bitcast(dt.uint32), sc.bitcast(dt.uint32).indirect(off[:, 0:8])))
         wait("s", *ready_s)
-        b = S(s.activation(ds[:, 0:K], ss.indirect(off[:, 0:8]), COPY))
+        b = S(s.activation(ds, ss.indirect(off[:, 0:8]), COPY))
         return a, b
 
-    def send(buf_c, buf_s, a, b, dst, sem_c, sem_s):
+    def send(out_c, in_c, out_s, in_s, a, b, dst, sem_c, sem_s):
         rid, pid = topo.addr(dst, core)
         m = topo.mask(core, dst)
         n = len(topo.engines(core, dst))
-        for buf, k, sem in ((buf_c, a, sem_c), (buf_s, b, sem_s)):
+        for o, i, k, sem in ((out_c.bitcast(dt.uint8), in_c.bitcast(dt.uint8), a, sem_c), (out_s, in_s, b, sem_s)):
             wait("g", k)
-            o, i = buf[:, K:2 * K], buf[:, 0:K]
-            if buf is buf_c:
-                o, i = o.bitcast(dt.uint8), i.bitcast(dt.uint8)
             g.remote_dma(o, i, T.sem[sem], T.sem["sent"], pid, rid, m)
             count["sent"] = count.get("sent", 0) + n
         return (sem_c, n), (sem_s, n)
 
-    k_l1 = invert("1", (k_pu,), 4, T.vals1, 384 if odd else 0, 2.0)
-    a1, b1 = pick(T.c1, T.s1, T.xq[:, 0:512], T.xs[:, 0:512], T.lst1, (k_l1,), (k_l1,))
+    def number_constants():
+        V(v.tensor_scalar(T.gm[:, 0:8], T.i6[:, 0:8], T.pcf[:, 0:1], None, OP.is_equal))
+        V(v.tensor_scalar(T.pct[:, 0:1], T.pt[:, 0:1], 128.0 * P + 512.0 * rank / GID, None, OP.add))
+    wait("v", k_i6, k_pt)
+    k_l1 = invert("1", (k_pu,), 4, 512, T.vals1, 384 if odd else 0, 2.0, number_constants)
+    a1, b1 = pick(T.c1[:, 0:K], T.s1[:, 0:K], T.xq[:, 0:512], T.xs[:, 0:512], T.lst1, (k_l1,), (k_l1,))
     mate = T.cores[rank ^ 1]
-    in1c, in1s = send(T.c1, T.s1, a1, b1, mate, "h1c", "h1s")
+    in1c, in1s = send(T.c1[:, K:2 * K], T.c1[:, 0:K], T.s1[:, K:2 * K], T.s1[:, 0:K], a1, b1, mate, "h1c", "h1s")
 
     m0 = 8 * rank
     wait("t", a1, b1)
     kaf = X(t.matmul_mx(T.psf[:, 0:128], T.uq[:, 0:128], T.us[:, 0:128], T.c1[:, 0:128], T.s1[:, 0:128], True, True))
-    kap = X(t.matmul_mx(T.psp[:, 0:128], T.c1[:, 0:128], T.s1[:, 0:128], T.uq[:, 0:128], T.us[:, 0:128], True, True))
-    wait("v", k_i6)
-    V(v.tensor_scalar(T.gm[:, 0:8], T.i6[:, 0:8], T.pcf[:, 0:1], None, OP.is_equal))
-    a = V(v.tensor_copy(T.o1f[:, 0:8], T.lst1[:, 0:8]))
+    kap = X(t.matmul_mx(T.psp[:, 0:128], T.c1[:, 0:128], T.s1[:, 0:128], T.uq0[:, 0:128], T.us0[:, 0:128], True, True))
+    a = V(v.tensor_scalar(T.o1f[:, 0:8], T.lst1[:, 0:8], 1.0 / GID, T.pct[:, 0:1], OP.mult, OP.add))
     wait("v", a)
     a = V(v.tensor_tensor(T.o1g[:, 0:8], T.o1f[:, 0:8], T.gm[:, 0:8], OP.mult))
+    wait("s", kap)
+    k_m4 = S(s.activation(T.msg[:, m0 + 4:m0 + 5], T.psp[:, 0:1], COPY))
     wait("v", a, kaf)
     a2 = V(v.transpose(T.at[:, 0:128], T.psf[:, 0:128]))
     V(v.tensor_reduce(T.msg[:, m0 + 5:m0 + 6], T.o1g[:, 0:8], AxisListType.X, OP.add))
-    wait("v", kap)
-    V(v.tensor_copy(T.msg[:, m0 + 4:m0 + 5], T.psp[:, 0:1]))
     wait("v", a2)
     k_msg = V(v.tensor_copy(T.msg[:, m0:m0 + 4], T.at[:, 0:128:32]))
-    wait("g", k_msg)
-    ids, m = [], topo.mask(core, T.cores[rank ^ 2])
-    for other in (rank ^ 2, rank ^ 3):
+    wait("g", k_msg, k_m4)
+    ids, m = [], topo.mask(core, mate)
+    for other in (rank ^ 2, rank ^ 3, rank ^ 1):
         dst = T.cores[other]
         rid, pid = topo.addr(dst, core)
         ids.append(DstId(rid=rid, pnc=pid))
         m &= topo.mask(core, dst)
     n = bin(m).count("1")
     view = T.msg[:, m0:m0 + 6]
-    g.remote_dma_fused([RemoteDMATransfer(dst_ids=ids, dma_engine_mask=m, remote_sem=T.sem["hm"], srcs=[view], dsts=[view] * 2)],
+    g.remote_dma_fused([RemoteDMATransfer(dst_ids=ids, dma_engine_mask=m, remote_sem=T.sem["hm"], srcs=[view], dsts=[view] * 3)],
                        local_sem=T.sem["sent"])
-    in_msg = ("hm", 2 * n)
-    rid, pid = topo.addr(mate, core)
-    view = T.msg[:, m0 + 5:m0 + 6]
-    g.remote_dma(view, view, T.sem["hp"], T.sem["sent"], pid, rid, topo.mask(core, mate))
-    in_num = ("hp", len(topo.engines(core, mate)))
-    count["sent"] += n + in_num[1]
+    in_msg = ("hm", 3 * n)
+    count["sent"] += n
 
-    a = V(v.tensor_scalar(T.mk[:, 0:128], T.ita[:, 0:128], 0.0, None, OP.is_equal))
+    a = V(v.tensor_scalar(T.nb0[:, 0:128], T.ita[:, 0:128], 0.0, 2 * BIG, OP.is_equal, OP.mult))
     b = V(v.memset(T.hs[:, 0:128], 0.0))
+    k = V(v.tensor_scalar(T.pcq[:, 1:2], T.pcf[:, 1:2], 128.0, None, OP.add))
     wait("v", a)
-    a = V(v.tensor_scalar(T.nb[:, 0:128], T.mk[:, 0:128], BIG, -BIG, OP.mult, OP.add))
-    b2 = V(v.tensor_tensor(T.am0[:, 0:128], T.psf[:, 0:128], T.mk[:, 0:128], OP.mult))
-    wait("v", a, b2)
-    k_am = V(v.tensor_tensor(T.am[:, 0:128], T.am0[:, 0:128], T.nb[:, 0:128], OP.add))
+    a = V(v.tensor_scalar(T.nb[:, 0:128], T.nb0[:, 0:128], -BIG, None, OP.add))
+    wait("v", b, k)
     k_hs = V(v.tensor_scalar(T.hs[:, 0:128:16], T.i6[:, 0:8], T.pcq[:, 1:2], 1.0 / 128, OP.add, OP.mult))
-    wait("v", k_i5, k_i7)
-    k_eo = V(v.tensor_copy(T.eoff[:, 0:16], T.i5[:, 0:16]))
-    V(v.tensor_scalar(T.hm[:, 0:32], T.i7[:, 0:32], T.pcf[:, 2:3], None, OP.is_equal))
-    V(v.memset(T.win2[:, 0:512], 0.0))
-    V(v.memset(T.ti2[:, 0:32], 0.0))
-    ca, cb, cx = (T.ca0, T.ca1), (T.cb0, T.cb1), (T.cx0, T.cx1)
-    for j in range(2):
-        V(v.tensor_scalar(T.pos[:, j:j + 1], T.pcf[:, 3:4], 128.0 * j + 1024.0 * (pair ^ j) / GID, None, OP.add))
-        V(v.tensor_copy(ca[j][:, 128:129], T.pcf[:, 3:4]))
-        V(v.tensor_scalar(cb[j][:, 128:129], T.pcf[:, 3:4], -1.0, 127.0, OP.mult, OP.add))
+    wait("v", a)
+    k_am = V(v.tensor_tensor(T.am[:, 0:128], T.nb[:, 0:128], T.psf[:, 0:128], OP.min))
     wait("v", dw)
     k_w = V(v.quantize_mx(T.wq[:, 0:256], T.ws[:, 0:256], T.wb[:, 0:1024]))
+    wait("v", k_i5, k_i7)
+    V(v.tensor_copy(T.eoff[:, 0:16], T.i5[:, 0:16]))
+    V(v.tensor_scalar(T.hm[:, 0:32], T.i7[:, 0:32], T.pcf[:, 2:3], None, OP.is_equal))
+    k_co = V(v.tensor_scalar(T.pct[:, 1:2], T.pt[:, 0:1], -2.0, 127.0, OP.mult, OP.add))
+    V(v.memset(T.win2[:, 0:384], 0.0))
+    V(v.memset(T.ti2[:, 0:32], 0.0))
 
+    word = lambda rk, w: T.msg[:, 8 * rk + w:8 * rk + w + 1]
+    E, O = T.msg[:, 4:32:16], T.msg[:, 12:32:16]
+    ps, sel, nsel = [[T[b][:, j:j + 1] for j in range(2)] for b in ("ps", "sel", "nsel")]
+    fr = (T.psf[:, 512:640], T.psf[:, 0:128]) if odd else (T.psf[:, 0:128], T.psf[:, 512:640])
+    wait("s", in_msg, k_co)
+    ky = S(s.activation(T.yx[:, 0:256], T.msg[:, 16 * Q:16 * Q + 16].indirect(T.eoff[:, 0:16]), COPY))
     wait("t", in1c, in1s)
     kb = X(t.matmul_mx(T.psf[:, 512:640], T.uq[:, 0:128], T.us[:, 0:128], T.c1[:, 128:256], T.s1[:, 128:256], True, True))
-    kbp = X(t.matmul_mx(T.psp[:, 512:640], T.c1[:, 128:256], T.s1[:, 128:256], T.uq[:, 0:128], T.us[:, 0:128], True, True))
     wait("v", kb, k_am)
     a = V(v.tensor_tensor(T.bc[:, 0:128], T.am[:, 0:128], T.psf[:, 512:640], OP.is_gt if odd else OP.is_ge))
+    wait("v", in_msg, k_m4)
+    V(v.tensor_tensor(T.ps[:, 0:2], E, O, OP.max))
+    V(v.tensor_tensor(T.sel[:, 0:2], O, E, OP.is_gt))
     wait("v", a, k_hs)
     a = V(v.tensor_tensor_scan(T.bs[:, 0:128], T.hs[:, 0:128], T.bc[:, 0:128], 0.0, OP.max, OP.subtract))
+    V(v.tensor_tensor(T.nsel[:, 0:2], E, O, OP.is_ge))
+    k_vd = V(v.tensor_tensor(T.vd[:, 0:2], T.msg[:, 13:32:16], T.msg[:, 5:32:16], OP.subtract))
     wait("v", a)
     k_o2 = V(v.tensor_scalar(T.off2[:, 0:8], T.bs[:, 15:128:16], 128.0, None, OP.mult))
-    a2, b2 = pick(T.c2, T.s2, T.c1[:, 0:256], T.s1[:, 0:256], T.off2, (k_o2, in1c), (k_o2, in1s))
-    in2c, in2s = send(T.c2, T.s2, a2, b2, T.cores[rank ^ 2], "h2c", "h2s")
+    wait("v", k_vd)
+    cmp(T.ba[:, 0:128], fr[1], ps[P], OP.is_gt, nsel[P])
+    a2, b2 = pick(T.c2[:, own], T.s2[:, own], T.c1[:, 0:256], T.s1[:, 0:256], T.off2, (k_o2, in1c), (k_o2, in1s))
+    in2c, in2s = send(T.c2[:, own], T.c2[:, own], T.s2[:, own], T.s2[:, own], a2, b2, T.cores[rank ^ 2], "h2c", "h2s")
 
-    j1 = pair ^ 1
-    wait("s", in_msg, k_eo)
-    ky = S(s.activation(T.yx[:, 0:256], T.msg[:, 16 * j1:16 * j1 + 16].indirect(T.eoff[:, 0:16]), COPY))
-    ps, sel = [T.ps[:, j:j + 1] for j in range(2)], [T.sel[:, j:j + 1] for j in range(2)]
-    acc = [T.acc[:, j:j + 1] for j in range(6)]
-    mine, his = T.msg[:, m0 + 4:m0 + 5], T.psp[:, 512:513]
-    fr = (T.psf[:, 512:640], T.psf[:, 0:128]) if odd else (T.psf[:, 0:128], T.psf[:, 512:640])
-    wait("v", kbp)
-    V(v.tensor_tensor(ps[0], his, mine, OP.max))
-    a = V(v.tensor_tensor(sel[0], his, mine, OP.is_lt if odd else OP.is_gt))
-    wait("v", a)
-    a = cmp(ca[0][:, 0:128], fr[1], ps[0], OP.is_gt)
-    b = cmp(cb[0][:, 0:128], fr[0], ps[0], OP.is_ge)
-    ka = [None] * 6
-    ka[0] = total(ca[0], 0, 129, acc[0], a)
-    ka[1] = total(cb[0], 0, 129, acc[1], b)
-    col = lambda c, w: T.msg[:, 8 * c + w:8 * c + w + 1]
-    wait("v", in_msg)
-    V(v.tensor_tensor(ps[1], col(2 * j1, 4), col(2 * j1 + 1, 4), OP.max))
-    a = V(v.tensor_tensor(sel[1], col(2 * j1 + 1, 4), col(2 * j1, 4), OP.is_gt))
-    wait("v", a)
-    for f in range(2):
-        k = cmp(cx[1][:, 128 * f:128 * f + 128], fr[f], ps[1], OP.is_ge if pair == 0 else OP.is_gt)
-    ka[5] = total(cx[1], 0, 256, acc[5], k)
+    def products(side, bank, *ready):
+        wait("t", k_w, *ready)
+        return [X(t.matmul_mx(bank[:, 512 * (o + 2):512 * (o + 2) + 128], T.wq[:, 128 * o:128 * o + 128], T.ws[:, 128 * o:128 * o + 128],
+                              T.c2[:, side], T.s2[:, side], True, True)) for o in range(2)]
+    ko = products(own, T.psf, a2, b2)
+    kr = products(arr, T.psp, in2c, in2s)
+
+    wait("s", k_vd)
+    for j, buf in ((P, T.ba), (Q, T.bb)):
+        kc = S(s.activation(buf[:, 256:257], sel[j], IDENT, bias=T.pt[:, 0:1], scale=T.pct[:, 1:2]))
+    a = cmp(T.ba[:, 128:256], fr[0], ps[P], OP.is_ge, sel[P])
+    ka = total(T.ba, 0, 257, T.ba[:, 257:258], a, kc)
+    for j in range(2):
+        kcp = S(s.activation(T.cp[:, j:j + 1], T.vd[:, j:j + 1], IDENT, bias=word(2 * j, 5), scale=sel[j]))
     wait("v", ky)
-    k = V(v.transpose(T.fs[:, 0:256], T.yx[:, 0:256]))
-    wait("v", in_num)
-    for j in range(2):
-        b = V(v.tensor_scalar(T.cp0[:, j:j + 1], col(2 * (pair ^ j) + 1, 5), col(2 * (pair ^ j), 5), 512.0, OP.subtract, OP.add))
-    wait("v", k)
-    k = cmp(cx[0][:, 0:256], T.fs[:, 0:256], ps[0], OP.is_ge if pair == 1 else OP.is_gt)
-    ka[4] = total(cx[0], 0, 256, acc[4], k)
-    wait("v", b)
-    for j in range(2):
-        b = V(v.tensor_scalar(T.cp1[:, j:j + 1], T.cp0[:, j:j + 1], sel[j], col(2 * (pair ^ j), 5), OP.mult, OP.add))
-    k = cmp(ca[1][:, 0:128], T.fs[:, 128:256], ps[1], OP.is_gt)
-    ka[2] = total(ca[1], 0, 129, acc[2], k)
-    wait("v", b)
-    for j in range(2):
-        kcp = V(v.tensor_scalar(T.cp[:, j:j + 1], T.cp1[:, j:j + 1], 1.0 / GID, T.pos[:, j:j + 1], OP.mult, OP.add))
-    k = cmp(cb[1][:, 0:128], T.fs[:, 0:128], ps[1], OP.is_ge)
+    kt = V(v.transpose(T.fs[:, 0:256], T.yx[:, 0:256]))
+    for f in range(2):
+        k = cmp(T.bb[:, 128 * f:128 * f + 128], fr[f], ps[Q], OP.is_ge if P < Q else OP.is_gt)
     wait("s", kcp)
     for j in range(2):
         kz = S(s.activation(T.zx[:, 32 * j:32 * j + 32], T.hm[:, 0:32], COPY, scale=T.cp[:, j:j + 1]))
-    ka[3] = total(cb[1], 0, 129, acc[3], k)
-    wait("v", ka[0], ka[1])
-    V(v.tensor_scalar(T.dd[:, 0:1], acc[1], acc[0], sel[0], OP.subtract, OP.mult))
+    kb = total(T.bb, 0, 257, T.bb[:, 257:258], k)
+    wait("v", kt)
+    k = cmp(T.ba[:, 258:514], T.fs[:, 0:256], ps[P], OP.is_ge if Q < P else OP.is_gt)
+    ka = total(T.ba, 257, 514, T.pl2[:, P:P + 1], k, ka)
+    k = cmp(T.bb[:, 258:386], T.fs[:, 128:256], ps[Q], OP.is_gt, nsel[Q])
+    kb = total(T.bb, 257, 386, T.bb[:, 514:515], k, kb)
+    k = cmp(T.bb[:, 386:514], T.fs[:, 0:128], ps[Q], OP.is_ge, sel[Q])
     wait("v", kz)
     a = V(v.transpose(T.zt[:, 0:64], T.zx[:, 0:64]))
-    wait("v", ka[2], ka[3])
-    b = V(v.tensor_scalar(T.dd[:, 1:2], acc[3], acc[2], sel[1], OP.subtract, OP.mult))
     wait("v", a)
     for j in range(2):
         V(v.tensor_tensor(T.vals2[:, 16 * j:16 * j + 16], T.zt[:, 32 * j:32 * j + 16], T.zt[:, 32 * j + 16:32 * j + 32], OP.add))
-    wait("v", b, ka[4], ka[5])
-    for j in range(2):
-        kv = V(v.tensor_scalar(T.pu2[:, j:j + 1], T.dd[:, j:j + 1], acc[2 * j], acc[4 + j], OP.add, OP.add))
-    k_l2 = invert("2", (kv,), 2, T.vals2, 0, 1.0)
+    wait("v", k, kb)
+    a = V(v.tensor_reduce(T.pl2[:, Q:Q + 1], T.bb[:, 386:515], AxisListType.X, OP.add))
+    wait("v", a, ka)
+    kv = V(v.tensor_copy(T.pu2[:, 0:2], T.pl2[:, 0:2]))
 
-    a3, b3 = pick(T.c3, T.s3, T.c2[:, 0:256], T.s2[:, 0:256], T.lst2, (k_l2, in2c), (k_l2, in2s))
-    wait("t", a3, b3, k_w)
-    ko = [X(t.matmul_mx(T.psp[:, 512 * (o + 2):512 * (o + 2) + 128], T.wq[:, 128 * o:128 * o + 128], T.ws[:, 128 * o:128 * o + 128],
-                        T.c3[:, 0:128], T.s3[:, 0:128], True, True)) for o in range(2)]
-    a = V(v.tensor_scalar(T.idn[0:32, 0:16], T.tw2[0:32, 0:16], float(GID), None, OP.mult))
+    yw = (T.yw0, T.yw1)
+    for side, bank, kk in ((own, T.psf, ko), (arr, T.psp, kr)):
+        for o in range(2):
+            wait("s", kk[o])
+            kyw = S(s.activation(yw[o][:, side], bank[:, 512 * (o + 2):512 * (o + 2) + 128], COPY))
+
+    def numbers():
+        V(v.tensor_scalar(T.idn[0:32, 0:16], T.tw2[0:32, 0:16], float(GID), None, OP.mult))
+    k_l2 = invert("2", (kv,), 2, 384, T.vals2, 0, 1.0, numbers)
+
+    wait("v", k_l2, kyw)
+    ky0 = V(v.tensor_copy(T.yb0[:, 0:128], T.yw0[:, 0:256].indirect(T.lst2[:, 0:8])))
+    wait("s", k_l2, kyw)
+    ky1 = S(s.activation(T.yb1[:, 0:128], T.yw1[:, 0:256].indirect(T.lst2[:, 0:8]), COPY))
+    wait("s", ky1)
+    d1 = done(s.dma_start(T.y[:, 128:256], T.yb1[:, 0:128]), "dy1", 16)
+    wait("y", ky0)
+    d0 = done(y.dma_start(T.y[:, 0:128], T.yb0[:, 0:128]), "dy0", 16)
+    V(v.tensor_scalar(T.idi[0:32, 0:16], T.idn[0:32, 0:16], 9, 3, OP.arith_shift_right, OP.bitwise_and))
+    a = V(v.tensor_scalar(T.idi[0:32, 16:32], T.idn[0:32, 0:16], 511, None, OP.bitwise_and))
     wait("v", a)
-    V(v.tensor_scalar(T.idr[0:32, 0:16], T.idn[0:32, 0:16], 9, 3, OP.arith_shift_right, OP.bitwise_and))
-    a = V(v.tensor_scalar(T.idc[0:32, 0:16], T.idn[0:32, 0:16], 511, None, OP.bitwise_and))
-    wait("v", a)
-    V(v.tensor_copy(T.idf[0:32, 0:16], T.idr[0:32, 0:16]))
-    kid = V(v.tensor_copy(T.idf[0:32, 16:32], T.idc[0:32, 0:16]))
-    wait("s", ko[0])
-    ky0 = S(s.activation(T.yb[:, 0:128], T.psp[:, 1024:1152], COPY))
-    wait("v", ko[1])
-    ky1 = V(v.tensor_copy(T.yb[:, 128:256], T.psp[:, 1536:1664]))
-    wait("s", ky0)
-    d0 = done(s.dma_start(T.y[:, 0:128], T.yb[:, 0:128]), "dy0", 16)
+    kid = V(v.tensor_copy(T.idf[0:32, 0:32], T.idi[0:32, 0:32]))
     wait("y", kid)
     for row in range(2):
         d2 = done(y.dma_start(T["id"][row:row + 1, 0:128], T.idf[0:8, 16 * row:16 * row + 16]), "did", 16)
-    wait("y", ky1)
-    d1 = done(y.dma_start(T.y[:, 128:256], T.yb[:, 128:256]), "dy1", 16)
-    wait("g", ("sent", count["sent"]), in1c, in1s, in2c, in2s, in_msg, in_num, du, *dx, dw,
+    wait("g", ("sent", count["sent"]), in1c, in1s, in2c, in2s, in_msg, du, *dx, dw,
          ("gc", count["gc"]), ("v", count["v"]), ("s", count["s"]), ("t", count["t"]), d0, d1, d2)

from concourse.bass import DstId, RemoteDMATransfer
from concourse.mybir import dt, AluOpType, AxisListType, ActivationFunctionType

OP = AluOpType
COPY = ActivationFunctionType.Copy
IDENT = ActivationFunctionType.Identity
SQUARE = ActivationFunctionType.Square
K = 128
BIG = 1e29
LIFT = 256.0
GID = 4096

SCRATCH = {
    "ur": ("sbuf", [128, 512], "bfloat16"), "zoff": ("sbuf", [128, 8], "uint16"),
    "uq0": ("sbuf", [128, 128], "float8_e4m3fn_x4"), "us0": ("sbuf", [128, 128], "uint8"),
    "uq": ("sbuf", [128, 128], "float8_e4m3fn_x4"), "us": ("sbuf", [128, 128], "uint8"),
    "xb": ("sbuf", [128, 2048], "bfloat16"),
    "xq": ("sbuf", [128, 512], "float8_e4m3fn_x4"), "xs": ("sbuf", [128, 512], "uint8"),
    "wb": ("sbuf", [128, 1024], "bfloat16"),
    "wq": ("sbuf", [128, 256], "float8_e4m3fn_x4"), "ws": ("sbuf", [128, 256], "uint8"),
    "c1": ("sbuf", [128, 256], "float8_e4m3fn_x4"), "s1": ("sbuf", [128, 256], "uint8"),
    "c2": ("sbuf", [128, 256], "float8_e4m3fn_x4"), "s2": ("sbuf", [128, 256], "uint8"),
    "yw0": ("sbuf", [128, 256], "float32"), "yw1": ("sbuf", [128, 256], "float32"),
    "yb0": ("sbuf", [128, 128], "float32"), "yb1": ("sbuf", [128, 128], "float32"),
    "psf": ("psum", [128, 2048], "float32"),
    "psp": ("psum", [128, 2048], "float32"),
    "ip": ("sbuf", [128, 4], "int32"), "pt": ("sbuf", [128, 4], "float32"),
    "it": ("sbuf", [128, 128], "int32"), "ita": ("sbuf", [128, 128], "int32"),
    "nb0": ("sbuf", [128, 128], "float32"), "nb": ("sbuf", [128, 128], "float32"),
    "ch0": ("sbuf", [128, 128], "float32"), "ch1": ("sbuf", [128, 128], "float32"), "ch": ("sbuf", [128, 128], "float32"),
    "i3": ("sbuf", [128, 64], "float32"), "vals1": ("sbuf", [128, 64], "float32"),
    "i5": ("sbuf", [128, 16], "int32"), "eoff": ("sbuf", [128, 16], "uint16"),
    "i6": ("sbuf", [128, 8], "float32"), "gm": ("sbuf", [128, 8], "float32"), "hs": ("sbuf", [128, 128], "float32"),
    "i7": ("sbuf", [128, 32], "float32"), "hm": ("sbuf", [128, 32], "float32"),
    "pca": ("sbuf", [128, 3], "int32"), "pcf": ("sbuf", [128, 3], "float32"), "pcq": ("sbuf", [128, 2], "float32"),
    "pct": ("sbuf", [128, 2], "float32"),
    "sf": ("sbuf", [128, 512], "float32"), "sm": ("sbuf", [128, 512], "float32"),
    "cma": ("sbuf", [128, 648], "float32"), "cmb": ("sbuf", [128, 648], "float32"),
    "cmc": ("sbuf", [128, 648], "float32"), "cmd": ("sbuf", [128, 648], "float32"),
    "junk": ("sbuf", [128, 4096], "bfloat16"),
    "pl1": ("sbuf", [128, 4], "float32"),
    "msg": ("sbuf", [128, 32], "float32"),
    "at": ("sbuf", [128, 128], "float32"), "o1f": ("sbuf", [128, 8], "float32"), "o1g": ("sbuf", [128, 8], "float32"),
    "am": ("sbuf", [128, 128], "float32"),
    "bc": ("sbuf", [128, 128], "float32"), "bs": ("sbuf", [128, 128], "float32"),
    "off2": ("sbuf", [128, 8], "uint16"),
    "yx": ("sbuf", [128, 256], "float32"), "fs": ("sbuf", [128, 256], "float32"),
    "ps": ("sbuf", [128, 2], "float32"), "sel": ("sbuf", [128, 2], "float32"), "nsel": ("sbuf", [128, 2], "float32"),
    "vd": ("sbuf", [128, 2], "float32"), "cp": ("sbuf", [128, 2], "float32"),
    "ba": ("sbuf", [128, 520], "float32"), "bb": ("sbuf", [128, 520], "float32"),
    "pl2": ("sbuf", [128, 2], "float32"),
    "zx": ("sbuf", [128, 64], "float32"), "zt": ("sbuf", [128, 64], "float32"),
    "vals2": ("sbuf", [128, 32], "float32"),
    "idn": ("sbuf", [32, 16], "int32"), "idi": ("sbuf", [32, 32], "int32"), "idf": ("sbuf", [32, 32], "float32"),
}
for _n in ("1", "2"):
    SCRATCH["pu" + _n] = ("sbuf", [128, 4], "uint16")
    SCRATCH["win" + _n] = ("sbuf", [128, 512], "float32")
    SCRATCH["sc" + _n] = ("sbuf", [128, 128], "float32")
    SCRATCH["qa" + _n] = ("sbuf", [64, 8], "float32")
    for _b in ("ti", "to", "tw", "tb"):
        SCRATCH[_b + _n] = ("sbuf", [32, 32], "float32")
    SCRATCH["lst" + _n] = ("sbuf", [128, 8], "uint16")

SEMAPHORES = ["v", "s", "t", "gc", "du", "dx0", "dx1", "dx2", "dx3", "dw", "dy0", "dy1", "did",
              "h1c", "h1s", "h2c", "h2s", "hm", "sent"]


def rank_program(g, core, T, topo):
    rank = T.rank_of(core)
    if rank is None:
        return
    v, s, t, y = g.vector, g.scalar, g.tensor, g.sync
    queue = {"g": g, "v": v, "s": s, "t": t, "y": y}
    count, waited = {}, {}
    odd, P, Q = rank % 2, rank // 2, (rank // 2) ^ 1
    own, arr = slice(K * P, K * P + K), slice(K * Q, K * Q + K)

    def done(ins, sem, n=1):
        ins.then_inc(T.sem[sem], n)
        count[sem] = count.get(sem, 0) + n
        return (sem, count[sem])

    def wait(q, *tokens):
        best = {}
        for sem, n in tokens:
            best[sem] = max(best.get(sem, 0), n)
        for sem, n in best.items():
            if waited.get((q, sem), 0) < n:
                waited[(q, sem)] = n
                queue[q].wait_ge(T.sem[sem], n)

    def V(ins): return done(ins, "v")
    def S(ins): return done(ins, "s")
    def X(ins): return done(ins, "t")

    du = done(s.dma_start(T.ur[:, 0:8], T.u[:, 0:8]), "du", 16)
    dx = [done(y.dma_start(T.xb[:, 512 * d:512 * d + 512], T.x[:, 512 * d:512 * d + 512]), "dx%d" % d, 16) for d in range(4)]
    dw = done(y.dma_start(T.wb[:, 0:1024], T.w[:, 0:1024]), "dw", 16)

    def iota(buf, pattern, base, cm, flt=False):
        if flt:
            return done(g.iota(buf, pattern, base, cm, allow_small_or_imprecise_dtypes=True), "gc")
        return done(g.iota(buf, pattern, base, cm), "gc")
    k_it = iota(T.it[:, 0:128], [[1, 128]], 128, -1)
    k_ip = iota(T.ip[:, 0:4], [[0, 4]], 0, 1)
    k_i3 = iota(T.i3[:, 0:64], [[128, 4], [1, 16]], 0, 0, True)
    k_i6 = iota(T.i6[:, 0:8], [[16, 8]], 0, 0, True)
    k_pt = iota(T.pt[:, 0:4], [[0, 4]], 0, 1, True)
    k_i5 = iota(T.i5[:, 0:16], [[8, 2], [1, 4], [0, 2]], 0, 0)
    k_i7 = iota(T.i7[:, 0:32], [[16, 2], [0, 16]], 0, 0, True)

    k_ur = V(v.memset(T.ur[:, 8:512], 0.0))
    k_zo = V(v.memset(T.zoff[:, 0:8], 0))
    V(v.memset(T.win1[:, 0:512], 0.0))
    wait("v", k_it)
    k = V(v.tensor_scalar(T.ita[:, 0:128], T.it[:, 0:128], 15, None, OP.bitwise_and))
    wait("v", k)
    k_d = V(v.tensor_scalar(T.ch0[:, 0:128], T.ita[:, 0:128], 2.0, None, OP.min))

    wait("v", du, k_ur)
    k_u0 = V(v.quantize_mx(T.uq0[:, 0:128], T.us0[:, 0:128], T.ur[:, 0:512]))
    wait("v", k_u0, k_zo)
    k_uc = V(v.tensor_copy(T.uq[:, 0:128].bitcast(dt.uint32), T.uq0[:, 0:128].bitcast(dt.uint32).indirect(T.zoff[:, 0:8])))
    wait("s", k_u0)
    k_us = S(s.activation(T.us[:, 0:128], T.us0[:, 0:128].indirect(T.zoff[:, 0:8]), COPY))
    k = S(s.activation(T.ch1[:, 0:128], T.ch0[:, 0:128], SQUARE, bias=-1.25))
    wait("s", k)
    k_ch = S(s.activation(T.ch[:, 0:128], T.ch1[:, 0:128], IDENT, bias=1.125 * LIFT, scale=-2 * LIFT))

    kq = [None] * 4

    def quant(d):
        e = slice(128 * d, 128 * d + 128)
        wait("v", dx[d])
        kq[d] = V(v.quantize_mx(T.xq[:, e], T.xs[:, e], T.xb[:, 512 * d:512 * d + 512]))
    quant(0)
    wait("v", k_ip)
    V(v.tensor_scalar(T.pca[:, 0:1], T.ip[:, 0:1], 112, None, OP.bitwise_and))
    V(v.tensor_scalar(T.pca[:, 1:2], T.ip[:, 0:1], 15, None, OP.bitwise_and))
    b = V(v.tensor_scalar(T.pca[:, 2:3], T.ip[:, 0:1], 16, None, OP.bitwise_and))
    quant(1)
    wait("v", b)
    b = V(v.tensor_copy(T.pcf[:, 0:3], T.pca[:, 0:3]))
    wait("v", b, k_i3)
    V(v.tensor_scalar(T.pcq[:, 0:1], T.pcf[:, 1:2], 15.0, -8 * LIFT, OP.is_lt, OP.mult))
    V(v.tensor_scalar(T.vals1[:, 0:64], T.i3[:, 0:64], T.pcf[:, 0:1], 0.5, OP.add, OP.mult))
    quant(2)

    kp, kh, kf, km = [None] * 4, [None] * 2, [None] * 4, [None] * 4

    def down(c):
        e = slice(128 * c, 128 * c + 128)
        wait("t", k_u0, kq[c])
        kp[c] = X(t.matmul_mx(T.psp[:, 512 * c:512 * c + 128], T.xq[:, e], T.xs[:, e], T.uq0[:, 0:128], T.us0[:, 0:128], True, True))

    def half(h):
        e = slice(256 * h, 256 * h + 256)
        wait("t", k_uc, k_us, kq[2 * h + 1])
        kh[h] = X(t.matmul_mx(T.psf[:, 512 * h:512 * h + 256], T.uq[:, 0:128], T.us[:, 0:128], T.xq[:, e], T.xs[:, e], True, True))

    def block(c):
        e = slice(128 * c, 128 * c + 128)
        o = 512 * (2 + c % 2)
        wait("t", k_uc, k_us, kq[c])
        if c > 1:
            wait("t", kf[c - 2])
        k = X(t.matmul_mx(T.psf[:, o:o + 128], T.uq[:, 0:128], T.us[:, 0:128], T.xq[:, e], T.xs[:, e], True, True))
        wait("s", k)
        kf[c] = S(s.activation(T.sf[:, e], T.psf[:, o:o + 128], COPY))
        wait("g", kf[c])
        km[c] = done(g.affine_select(T.sm[:, e], T.sf[:, e], [[-1, 128]], OP.is_gt, BIG, 0, 1), "gc")

    cm = [T.cma, T.cmb, T.cmc, T.cmd]
    jk = [0]

    def total(buf, lo, hi, out, *tokens):
        wait("s", *tokens)
        n = hi - lo
        r = S(s.activation(T.junk[:, jk[0]:jk[0] + n], buf[:, lo:hi], COPY, accum_out=out))
        jk[0] = jk[0] + n if jk[0] + n + 700 <= 4096 else 0
        return r

    def cmp(out, src, col, op, weight=None):
        if weight is None:
            return V(v.tensor_scalar(out, src, col, None, op))
        return V(v.tensor_scalar(out, src, col, weight, op, OP.mult))
    sp = [T.psp[:, 512 * c:512 * c + 1] for c in range(4)]
    h0, h1, sm = T.psf[:, 0:256], T.psf[:, 512:768], T.sm
    down(0)
    block(0)
    half(0)
    down(1)
    block(1)
    down(2)
    wait("v", kp[0], kh[0])
    cmp(cm[0][:, 0:256], h0, sp[0], OP.is_gt)
    quant(3)
    half(1)
    wait("v", kp[1])
    cmp(cm[1][:, 0:128], T.psf[:, 0:128], sp[1], OP.is_ge)
    k = cmp(cm[1][:, 128:256], T.psf[:, 128:256], sp[1], OP.is_gt)
    e1 = total(cm[1], 0, 256, cm[1][:, 256:257], k)
    wait("v", km[0])
    k = cmp(cm[0][:, 256:384], sm[:, 0:128], sp[0], OP.is_equal)
    e0 = total(cm[0], 0, 384, cm[0][:, 384:385], k)
    block(2)
    down(3)
    wait("v", kp[2])
    cmp(cm[2][:, 0:256], h0, sp[2], OP.is_ge)
    wait("v", kh[1])
    k = cmp(cm[2][:, 256:512], h1, sp[2], OP.is_gt)
    e2 = total(cm[2], 0, 512, cm[2][:, 512:513], k)
    k = cmp(cm[0][:, 385:641], h1, sp[0], OP.is_gt)
    block(3)
    total(cm[0], 384, 641, T.pl1[:, 0:1], k, e0)
    cmp(cm[1][:, 257:513], h1, sp[1], OP.is_gt)
    wait("v", km[1])
    k = cmp(cm[1][:, 513:641], sm[:, 128:256], sp[1], OP.is_equal)
    pl = total(cm[1], 256, 641, T.pl1[:, 1:2], k, e1)
    wait("v", kp[3])
    k = cmp(cm[3][:, 0:256], h0, sp[3], OP.is_ge)
    e3 = total(cm[3], 0, 256, cm[3][:, 640:641], k)
    cmp(cm[3][:, 256:384], T.psf[:, 512:640], sp[3], OP.is_ge)
    cmp(cm[3][:, 384:512], T.psf[:, 640:768], sp[3], OP.is_gt)
    wait("v", km[2])
    a = cmp(cm[2][:, 513:641], sm[:, 256:384], sp[2], OP.is_equal)
    wait("v", km[3])
    b = cmp(cm[3][:, 512:640], sm[:, 384:512], sp[3], OP.is_equal)
    V(v.memset(T.ti1[:, 0:32], 0.0))
    wait("v", a, e2)
    V(v.tensor_reduce(T.pl1[:, 2:3], cm[2][:, 512:641], AxisListType.X, OP.add))
    wait("v", b, e3)
    a = V(v.tensor_reduce(T.pl1[:, 3:4], cm[3][:, 256:641], AxisListType.X, OP.add))
    wait("v", a, pl)
    if odd:
        k_pu = V(v.tensor_scalar(T.pu1[:, 0:4], T.pl1[:, 0:4], -1.0, 511.0, OP.mult, OP.add))
    else:
        k_pu = V(v.tensor_copy(T.pu1[:, 0:4], T.pl1[:, 0:4]))

    def invert(n, ready, cols, width, vals, lo, scale, fill):
        W = lambda b: T[b + n]
        wait("v", k_ch, *ready)
        a = V(v.tensor_copy(W("win")[:, 0:width].indirect(W("pu")[:, 0:cols]), vals[:, 0:16 * cols]))
        wait("v", a)
        a = V(v.tensor_tensor_scan(W("sc")[:, 0:128], T.ch[:, 0:128], W("win")[:, lo:lo + 128], 0.0, OP.add, OP.max))
        wait("v", a)
        a = V(v.tensor_tensor(W("qa")[0:64, 0:8], W("sc")[0:64, 15:128:16], W("sc")[64:128, 15:128:16], OP.add))
        wait("v", a)
        a = V(v.tensor_tensor(W("ti")[0:32, 0:8], W("qa")[0:32, 0:8], W("qa")[32:64, 0:8], OP.add))
        wait("v", a)
        a = V(v.transpose(W("to")[0:32, 0:32], W("ti")[0:32, 0:32]))
        wait("v", a)
        V(v.tensor_tensor(W("tw")[0:32, 0:16], W("to")[0:32, 0:16], W("to")[0:32, 16:32], OP.add))
        a = V(v.tensor_tensor(W("tw")[0:32, 16:32], W("to")[0:32, 0:16], W("to")[0:32, 16:32], OP.add))
        wait("v", a)
        a = V(v.transpose(W("tb")[0:32, 0:32], W("tw")[0:32, 0:32]))
        fill()
        wait("v", a)
        for h in range(4):
            a = V(v.tensor_scalar(W("lst")[32 * h:32 * h + 32, 0:8], W("tb")[0:32, 0:8], T.pcq[0:32, 0:1], scale, OP.add, OP.mult))
        return a

    def pick(dc, ds, sc, ss, off, ready_c, ready_s):
        wait("v", *ready_c)
        a = V(v.tensor_copy(dc.bitcast(dt.uint32), sc.bitcast(dt.uint32).indirect(off[:, 0:8])))
        wait("s", *ready_s)
        b = S(s.activation(ds, ss.indirect(off[:, 0:8]), COPY))
        return a, b

    def send(out_c, in_c, out_s, in_s, a, b, dst, sem_c, sem_s):
        rid, pid = topo.addr(dst, core)
        m = topo.mask(core, dst)
        n = len(topo.engines(core, dst))
        for o, i, k, sem in ((out_c.bitcast(dt.uint8), in_c.bitcast(dt.uint8), a, sem_c), (out_s, in_s, b, sem_s)):
            wait("g", k)
            g.remote_dma(o, i, T.sem[sem], T.sem["sent"], pid, rid, m)
            count["sent"] = count.get("sent", 0) + n
        return (sem_c, n), (sem_s, n)

    def number_constants():
        V(v.tensor_scalar(T.gm[:, 0:8], T.i6[:, 0:8], T.pcf[:, 0:1], None, OP.is_equal))
        V(v.tensor_scalar(T.pct[:, 0:1], T.pt[:, 0:1], 128.0 * P + 512.0 * rank / GID, None, OP.add))
    wait("v", k_i6, k_pt)
    k_l1 = invert("1", (k_pu,), 4, 512, T.vals1, 384 if odd else 0, 2.0, number_constants)
    a1, b1 = pick(T.c1[:, 0:K], T.s1[:, 0:K], T.xq[:, 0:512], T.xs[:, 0:512], T.lst1, (k_l1,), (k_l1,))
    mate = T.cores[rank ^ 1]
    in1c, in1s = send(T.c1[:, K:2 * K], T.c1[:, 0:K], T.s1[:, K:2 * K], T.s1[:, 0:K], a1, b1, mate, "h1c", "h1s")

    m0 = 8 * rank
    wait("t", a1, b1)
    kaf = X(t.matmul_mx(T.psf[:, 0:128], T.uq[:, 0:128], T.us[:, 0:128], T.c1[:, 0:128], T.s1[:, 0:128], True, True))
    kap = X(t.matmul_mx(T.psp[:, 0:128], T.c1[:, 0:128], T.s1[:, 0:128], T.uq0[:, 0:128], T.us0[:, 0:128], True, True))
    a = V(v.tensor_scalar(T.o1f[:, 0:8], T.lst1[:, 0:8], 1.0 / GID, T.pct[:, 0:1], OP.mult, OP.add))
    wait("v", a)
    a = V(v.tensor_tensor(T.o1g[:, 0:8], T.o1f[:, 0:8], T.gm[:, 0:8], OP.mult))
    wait("s", kap)
    k_m4 = S(s.activation(T.msg[:, m0 + 4:m0 + 5], T.psp[:, 0:1], COPY))
    wait("v", a, kaf)
    a2 = V(v.transpose(T.at[:, 0:128], T.psf[:, 0:128]))
    V(v.tensor_reduce(T.msg[:, m0 + 5:m0 + 6], T.o1g[:, 0:8], AxisListType.X, OP.add))
    wait("v", a2)
    k_msg = V(v.tensor_copy(T.msg[:, m0:m0 + 4], T.at[:, 0:128:32]))
    wait("g", k_msg, k_m4)
    ids, m = [], topo.mask(core, mate)
    for other in (rank ^ 2, rank ^ 3, rank ^ 1):
        dst = T.cores[other]
        rid, pid = topo.addr(dst, core)
        ids.append(DstId(rid=rid, pnc=pid))
        m &= topo.mask(core, dst)
    n = bin(m).count("1")
    view = T.msg[:, m0:m0 + 6]
    g.remote_dma_fused([RemoteDMATransfer(dst_ids=ids, dma_engine_mask=m, remote_sem=T.sem["hm"], srcs=[view], dsts=[view] * 3)],
                       local_sem=T.sem["sent"])
    in_msg = ("hm", 3 * n)
    count["sent"] += n

    a = V(v.tensor_scalar(T.nb0[:, 0:128], T.ita[:, 0:128], 0.0, 2 * BIG, OP.is_equal, OP.mult))
    b = V(v.memset(T.hs[:, 0:128], 0.0))
    k = V(v.tensor_scalar(T.pcq[:, 1:2], T.pcf[:, 1:2], 128.0, None, OP.add))
    wait("v", a)
    a = V(v.tensor_scalar(T.nb[:, 0:128], T.nb0[:, 0:128], -BIG, None, OP.add))
    wait("v", b, k)
    k_hs = V(v.tensor_scalar(T.hs[:, 0:128:16], T.i6[:, 0:8], T.pcq[:, 1:2], 1.0 / 128, OP.add, OP.mult))
    wait("v", a)
    k_am = V(v.tensor_tensor(T.am[:, 0:128], T.nb[:, 0:128], T.psf[:, 0:128], OP.min))
    wait("v", dw)
    k_w = V(v.quantize_mx(T.wq[:, 0:256], T.ws[:, 0:256], T.wb[:, 0:1024]))
    wait("v", k_i5, k_i7)
    V(v.tensor_copy(T.eoff[:, 0:16], T.i5[:, 0:16]))
    V(v.tensor_scalar(T.hm[:, 0:32], T.i7[:, 0:32], T.pcf[:, 2:3], None, OP.is_equal))
    k_co = V(v.tensor_scalar(T.pct[:, 1:2], T.pt[:, 0:1], -2.0, 127.0, OP.mult, OP.add))
    V(v.memset(T.win2[:, 0:384], 0.0))
    V(v.memset(T.ti2[:, 0:32], 0.0))

    word = lambda rk, w: T.msg[:, 8 * rk + w:8 * rk + w + 1]
    E, O = T.msg[:, 4:32:16], T.msg[:, 12:32:16]
    ps, sel, nsel = [[T[b][:, j:j + 1] for j in range(2)] for b in ("ps", "sel", "nsel")]
    fr = (T.psf[:, 512:640], T.psf[:, 0:128]) if odd else (T.psf[:, 0:128], T.psf[:, 512:640])
    wait("s", in_msg, k_co)
    ky = S(s.activation(T.yx[:, 0:256], T.msg[:, 16 * Q:16 * Q + 16].indirect(T.eoff[:, 0:16]), COPY))
    wait("t", in1c, in1s)
    kb = X(t.matmul_mx(T.psf[:, 512:640], T.uq[:, 0:128], T.us[:, 0:128], T.c1[:, 128:256], T.s1[:, 128:256], True, True))
    wait("v", kb, k_am)
    a = V(v.tensor_tensor(T.bc[:, 0:128], T.am[:, 0:128], T.psf[:, 512:640], OP.is_gt if odd else OP.is_ge))
    wait("v", in_msg, k_m4)
    V(v.tensor_tensor(T.ps[:, 0:2], E, O, OP.max))
    V(v.tensor_tensor(T.sel[:, 0:2], O, E, OP.is_gt))
    wait("v", a, k_hs)
    a = V(v.tensor_tensor_scan(T.bs[:, 0:128], T.hs[:, 0:128], T.bc[:, 0:128], 0.0, OP.max, OP.subtract))
    V(v.tensor_tensor(T.nsel[:, 0:2], E, O, OP.is_ge))
    k_vd = V(v.tensor_tensor(T.vd[:, 0:2], T.msg[:, 13:32:16], T.msg[:, 5:32:16], OP.subtract))
    wait("v", a)
    k_o2 = V(v.tensor_scalar(T.off2[:, 0:8], T.bs[:, 15:128:16], 128.0, None, OP.mult))
    wait("v", k_vd)
    cmp(T.ba[:, 0:128], fr[1], ps[P], OP.is_gt, nsel[P])
    a2, b2 = pick(T.c2[:, own], T.s2[:, own], T.c1[:, 0:256], T.s1[:, 0:256], T.off2, (k_o2, in1c), (k_o2, in1s))
    in2c, in2s = send(T.c2[:, own], T.c2[:, own], T.s2[:, own], T.s2[:, own], a2, b2, T.cores[rank ^ 2], "h2c", "h2s")

    def products(side, bank, *ready):
        wait("t", k_w, *ready)
        return [X(t.matmul_mx(bank[:, 512 * (o + 2):512 * (o + 2) + 128], T.wq[:, 128 * o:128 * o + 128], T.ws[:, 128 * o:128 * o + 128],
                              T.c2[:, side], T.s2[:, side], True, True)) for o in range(2)]
    ko = products(own, T.psf, a2, b2)
    kr = products(arr, T.psp, in2c, in2s)

    wait("s", k_vd)
    for j, buf in ((P, T.ba), (Q, T.bb)):
        kc = S(s.activation(buf[:, 256:257], sel[j], IDENT, bias=T.pt[:, 0:1], scale=T.pct[:, 1:2]))
    a = cmp(T.ba[:, 128:256], fr[0], ps[P], OP.is_ge, sel[P])
    ka = total(T.ba, 0, 257, T.ba[:, 257:258], a, kc)
    for j in range(2):
        kcp = S(s.activation(T.cp[:, j:j + 1], T.vd[:, j:j + 1], IDENT, bias=word(2 * j, 5), scale=sel[j]))
    wait("v", ky)
    kt = V(v.transpose(T.fs[:, 0:256], T.yx[:, 0:256]))
    for f in range(2):
        k = cmp(T.bb[:, 128 * f:128 * f + 128], fr[f], ps[Q], OP.is_ge if P < Q else OP.is_gt)
    wait("s", kcp)
    for j in range(2):
        kz = S(s.activation(T.zx[:, 32 * j:32 * j + 32], T.hm[:, 0:32], COPY, scale=T.cp[:, j:j + 1]))
    kb = total(T.bb, 0, 257, T.bb[:, 257:258], k)
    wait("v", kt)
    k = cmp(T.ba[:, 258:514], T.fs[:, 0:256], ps[P], OP.is_ge if Q < P else OP.is_gt)
    ka = total(T.ba, 257, 514, T.pl2[:, P:P + 1], k, ka)
    k = cmp(T.bb[:, 258:386], T.fs[:, 128:256], ps[Q], OP.is_gt, nsel[Q])
    kb = total(T.bb, 257, 386, T.bb[:, 514:515], k, kb)
    k = cmp(T.bb[:, 386:514], T.fs[:, 0:128], ps[Q], OP.is_ge, sel[Q])
    wait("v", kz)
    a = V(v.transpose(T.zt[:, 0:64], T.zx[:, 0:64]))
    wait("v", a)
    for j in range(2):
        V(v.tensor_tensor(T.vals2[:, 16 * j:16 * j + 16], T.zt[:, 32 * j:32 * j + 16], T.zt[:, 32 * j + 16:32 * j + 32], OP.add))
    wait("v", k, kb)
    a = V(v.tensor_reduce(T.pl2[:, Q:Q + 1], T.bb[:, 386:515], AxisListType.X, OP.add))
    wait("v", a, ka)
    kv = V(v.tensor_copy(T.pu2[:, 0:2], T.pl2[:, 0:2]))

    yw = (T.yw0, T.yw1)
    for side, bank, kk in ((own, T.psf, ko), (arr, T.psp, kr)):
        for o in range(2):
            wait("s", kk[o])
            kyw = S(s.activation(yw[o][:, side], bank[:, 512 * (o + 2):512 * (o + 2) + 128], COPY))

    def numbers():
        V(v.tensor_scalar(T.idn[0:32, 0:16], T.tw2[0:32, 0:16], float(GID), None, OP.mult))
    k_l2 = invert("2", (kv,), 2, 384, T.vals2, 0, 1.0, numbers)

    wait("v", k_l2, kyw)
    ky0 = V(v.tensor_copy(T.yb0[:, 0:128], T.yw0[:, 0:256].indirect(T.lst2[:, 0:8])))
    wait("s", k_l2, kyw)
    ky1 = S(s.activation(T.yb1[:, 0:128], T.yw1[:, 0:256].indirect(T.lst2[:, 0:8]), COPY))
    wait("s", ky1)
    d1 = done(s.dma_start(T.y[:, 128:256], T.yb1[:, 0:128]), "dy1", 16)
    wait("y", ky0)
    d0 = done(y.dma_start(T.y[:, 0:128], T.yb0[:, 0:128]), "dy0", 16)
    V(v.tensor_scalar(T.idi[0:32, 0:16], T.idn[0:32, 0:16], 9, 3, OP.arith_shift_right, OP.bitwise_and))
    a = V(v.tensor_scalar(T.idi[0:32, 16:32], T.idn[0:32, 0:16], 511, None, OP.bitwise_and))
    wait("v", a)
    kid = V(v.tensor_copy(T.idf[0:32, 0:32], T.idi[0:32, 0:32]))
    wait("y", kid)
    for row in range(2):
        d2 = done(y.dma_start(T["id"][row:row + 1, 0:128], T.idf[0:8, 16 * row:16 * row + 16]), "did", 16)
    wait("g", ("sent", count["sent"]), in1c, in1s, in2c, in2s, in_msg, du, *dx, dw,
         ("gc", count["gc"]), ("v", count["v"]), ("s", count["s"]), ("t", count["t"]), d0, d1, d2)
